import numpy as np
import ml_dtypes


def mxq(x, axis, fmt="e4m3"):
    dtype, down = {"e4m3": (ml_dtypes.float8_e4m3fn, 7), "e5m2": (ml_dtypes.float8_e5m2, 14)}[fmt]
    v = np.moveaxis(np.asarray(x, np.float32).astype(ml_dtypes.bfloat16).astype(np.float64), axis, -1)
    blocks = v.reshape(v.shape[:-1] + (-1, 32))
    amax = np.abs(blocks).max(-1, keepdims=True)
    byte = np.maximum(np.where(amax > 0, np.frexp(amax)[1] - 1 + 127, 0) - down, 1)
    scale = np.exp2(byte - 127.0)
    codes = (blocks / scale).astype(np.float32).astype(dtype).astype(np.float64)
    return np.moveaxis((codes * scale).reshape(v.shape), -1, axis)


WIDE = False


def mx_kscale(k):
    if not WIDE:
        return np.ones(k)
    levels = np.array([10, -10, 5, -5, 0])
    if k % 512:
        return np.exp2(np.random.permutation(np.resize(levels, k // 32))).repeat(32)
    a = np.empty((k // 512, 16))
    for p in range(k // 512):
        a[p, :8] = np.random.permutation(np.resize(levels, 8))
        for g in range(8):
            far = levels[np.abs(levels - a[p, g]) >= 10]
            a[p, g + 8] = far[np.random.randint(len(far))]
    return np.exp2(a.ravel()).repeat(32)


def f64(x):
    return np.asarray(x).astype(np.float64)


def striped(idx):
    return np.tile(idx.reshape(-1, 16).T, (8, 1)).astype(np.uint16)


def unstriped(offs):
    return offs[:16].T.reshape(-1).astype(np.int64)


E2M1 = np.array([0.0, 0.5, 1.0, 1.5, 2.0, 3.0, 4.0, 6.0, -0.0, -0.5, -1.0, -1.5, -2.0, -3.0, -4.0, -6.0])


def pack_weight(w, fmt):
    k, n = w.shape
    w = f64(np.asarray(w, np.float32).astype(ml_dtypes.bfloat16)).reshape(k // 32, 32, n)
    amax = np.abs(w).max(1)
    if fmt == "e4m3":
        byte = np.frexp(amax)[1] - 1 + 127 - 7
    else:
        mant, ex = np.frexp(amax / 6.0)
        byte = np.where(mant > 0.5, ex, ex - 1) + 127
    byte = np.clip(np.where(amax > 0, byte, 1), 1, 254)
    scaled = (w * np.exp2(127.0 - byte)[:, None, :]).reshape(k, n).astype(np.float32)
    by_word = np.ascontiguousarray(scaled.reshape(k // 512, 128, 4, n).transpose(0, 1, 3, 2))
    if fmt == "e4m3":
        words = by_word.astype(ml_dtypes.float8_e4m3fn).view(np.uint8)
    else:
        c = by_word.astype(ml_dtypes.float4_e2m1fn).view(np.uint8) & 0xF
        words = (c[..., 0::2] | (c[..., 1::2] << 4)).reshape(k // 512, 128, 2 * n)
    return np.ascontiguousarray(words), np.ascontiguousarray(byte.astype(np.uint8).reshape(k // 512, 16, n))


def unpack_weight(words, scales, fmt):
    g, _, n = scales.shape
    words = np.ascontiguousarray(words).reshape(g, 128, n, -1)
    if fmt == "e4m3":
        vals = words.view(ml_dtypes.float8_e4m3fn).astype(np.float64)
    else:
        nib = np.empty((g, 128, n, 4), np.uint8)
        nib[..., 0::2] = words & 0xF
        nib[..., 1::2] = words >> 4
        vals = E2M1[nib]
    vals = vals * np.repeat(np.exp2(scales.astype(np.float64) - 127.0), 8, axis=1)[..., None]
    return vals.transpose(0, 1, 3, 2).reshape(g * 512, n)


def gelu(v):
    return 0.5 * v * (1.0 + np.tanh(np.sqrt(2.0 / np.pi) * (v + 0.044715 * v**3)))


K, T, E, C, H, N = 1024, 1024, 6, 128, 512, 256
R = 4


def by_expert(wq, xq):
    return np.concatenate([wq[e].T @ xq[:, e * C:(e + 1) * C] for e in range(E)], axis=1)


def setup_inputs():
    n = np.random.standard_normal
    s = mx_kscale(K)[:, None]
    u = mx_kscale(H)
    slot_token = np.concatenate([r * (T // R) + np.random.permutation(T // R)[:C // R] for e in range(E) for r in range(R)])
    w1 = [pack_weight(m, "e2m1") for m in n((E, K, H)) / np.sqrt(K) / s[None]]
    w3 = [pack_weight(m, "e2m1") for m in n((E, K, H)) / np.sqrt(K) / s[None] * u[None, None, :]]
    w2 = [pack_weight(m, "e2m1") for m in n((E, H, N)) / np.sqrt(H) / u[None, :, None]]
    return {
        "xT": (n((K, T)) * s).astype(np.float32),
        "w1_words": np.stack([m[0] for m in w1]),
        "w1_scales": np.stack([m[1] for m in w1]),
        "w3_words": np.stack([m[0] for m in w3]),
        "w3_scales": np.stack([m[1] for m in w3]),
        "w2_words": np.stack([m[0] for m in w2]),
        "w2_scales": np.stack([m[1] for m in w2]),
        "offs": striped(slot_token),
    }


def reference(xT, w1_words, w1_scales, w3_words, w3_scales, w2_words, w2_scales, offs):
    idx = unstriped(offs)
    w1 = np.stack([unpack_weight(w1_words[e], w1_scales[e], "e2m1") for e in range(E)])
    w3 = np.stack([unpack_weight(w3_words[e], w3_scales[e], "e2m1") for e in range(E)])
    w2 = np.stack([unpack_weight(w2_words[e], w2_scales[e], "e2m1") for e in range(E)])
    xq = mxq(f64(xT)[:, idx], 0, "e4m3")
    h = gelu(by_expert(w1, xq))
    h = h * by_expert(w3, xq)
    y = by_expert(w2, mxq(h, 0, "e4m3"))
    return y.reshape(N, E, R, C // R).transpose(0, 2, 1, 3).reshape(N, E * C)

@@ -1,0 +1,191 @@
+from contextlib import ExitStack
+
+import concourse.mybir as mybir
+from concourse.masks import make_identity
+
+K, T, E, C, H, N = 1024, 1024, 6, 128, 512, 256
+R = 4
+S = E * C
+P = 128
+PASSES = K // 512
+RU = C // R
+
+F32 = mybir.dt.float32
+BF16 = mybir.dt.bfloat16
+I32 = mybir.dt.int32
+U32 = mybir.dt.uint32
+U16 = mybir.dt.uint16
+U8 = mybir.dt.uint8
+FP8X4 = mybir.dt.float8_e4m3fn_x4
+FP4X4 = mybir.dt.float4_e2m1fn_x4
+ACT = mybir.ActivationFunctionType
+MULT = mybir.AluOpType.mult
+
+FLOPS = 2 * S * (2 * K * H + H * N)
+
+CHUNK = 512
+V_TOKENS = {(0, 0): 192, (0, 1): 192, (1, 0): 192, (1, 1): 320}
+GATHER = 384
+FIRST = 4
+
+
+def tile_moe_eps_glu_gelu_kernel(
+    tc, xT, w1_words, w1_scales, w3_words, w3_scales, w2_words, w2_scales, offs, out
+):
+    nc = tc.nc
+    with ExitStack() as ctx:
+        keep = ctx.enter_context(tc.tile_pool(name="keep", bufs=1))
+        ring = ctx.enter_context(tc.tile_pool(name="ring", bufs=2))
+        psum = ctx.enter_context(tc.psum_pool(name="psum", bufs=2))
+
+        offsets = keep.tile([P, S // 16], U16, name="offsets")
+
+        s1 = keep.tile([P, E * PASSES, H], U8, name="s1", align_bytes=64)
+        s3 = keep.tile([P, E * PASSES, H], U8, name="s3", align_bytes=64)
+        s2 = keep.tile([P, E, N], U8, name="s2", align_bytes=64)
+        tb = [keep.tile([P, T], U8, name=f"tb{s}", align_bytes=64) for s in range(PASSES)]
+        zero = keep.tile([P, 1], F32, name="zero")
+        warm = keep.tile([P, 1], F32, name="warm")
+        nc.vector.memset(zero[:], 0.0)
+        for t in (s1, s3, s2):
+            nc.vector.memset(t[:].rearrange("p a b -> p (a b)").bitcast(I32), 0)
+        for t in tb:
+            nc.vector.memset(t[:].bitcast(I32), 0)
+        nc.scalar.activation(out=warm[:], in_=zero[:], func=ACT.Gelu_apprx_tanh)
+        ident = keep.tile([P, P], F32, name="ident")
+        make_identity(nc, ident[:])
+
+        raw = {}
+        for s in range(PASSES):
+            for c in range(T // CHUNK):
+                raw[s, c] = keep.tile([P, 4, CHUNK], F32, name=f"raw{s}{c}")
+                nc.sync.dma_start(
+                    out=raw[s, c][:],
+                    in_=xT[512 * s : 512 * (s + 1), CHUNK * c : CHUNK * (c + 1)].rearrange("(p j) w -> p j w", j=4),
+                )
+                if (s, c) == (0, 0):
+                    nc.sync.dma_start(offsets[:], offs)
+        for dst, src in ((s1, w1_scales), (s3, w3_scales), (s2, w2_scales)):
+            rows = src.bitcast(I32).rearrange("e s (q r) i -> r q (e s) i", r=4)
+            for r in range(4):
+                nc.sync.dma_start(out=dst[:].bitcast(I32)[r:P:32], in_=rows[r])
+        w1 = [keep.tile([P, PASSES, 2 * H], U8, name=f"w1_{e}", align_bytes=64) for e in range(E)]
+        w3 = [keep.tile([P, PASSES, 2 * H], U8, name=f"w3_{e}", align_bytes=64) for e in range(E)]
+        w2 = [keep.tile([P, E // 2, 2 * N], U8, name=f"w2_{g}", align_bytes=64) for g in range(2)]
+        for e in range(E):
+            for dst, src in ((w1, w1_words), (w3, w3_words)):
+                nc.sync.dma_start(
+                    out=dst[e][:].bitcast(I32), in_=src[e].bitcast(I32).rearrange("s p b -> p s b")
+                )
+            if e in (0, 3):
+                g = e // 3
+                nc.sync.dma_start(
+                    out=w2[g][:].bitcast(I32),
+                    in_=w2_words[3 * g : 3 * g + 3].bitcast(I32).rearrange("e s p b -> p (e s) b"),
+                )
+
+        gw = [keep.tile([P, S], U32, name=f"gw{s}", align_bytes=64) for s in range(PASSES)]
+        gb = [keep.tile([P, S], U8, name=f"gb{s}", align_bytes=64) for s in range(PASSES)]
+        for s in range(PASSES):
+            tw = keep.tile([P, T], U32, name=f"tw{s}", align_bytes=64)
+            for c in range(T // CHUNK):
+                grouped = keep.tile([P, CHUNK, 4], BF16, name=f"grouped{s}{c}", align_bytes=64)
+                src = raw[s, c][:].rearrange("p j w -> p w j")
+                v = V_TOKENS[s, c]
+                nc.vector.tensor_copy(out=grouped[:, :v, :], in_=src[:, :v, :])
+                nc.scalar.activation(out=grouped[:, v:, :], in_=src[:, v:, :], func=ACT.Copy)
+                nc.vector.quantize_mx(
+                    out=tw[:, CHUNK * c : CHUNK * (c + 1)].bitcast(FP8X4),
+                    scales=tb[s][:, CHUNK * c : CHUNK * (c + 1)],
+                    in_=grouped[:].rearrange("p w j -> p (w j)"),
+                )
+            for g0 in range(0, S, GATHER):
+                idx = offsets[:, g0 // 16 : (g0 + GATHER) // 16]
+                nc.vector.tensor_copy(gw[s][:, g0 : g0 + GATHER], tw[:].indirect(idx))
+                nc.vector.tensor_copy(gb[s][:, g0 : g0 + GATHER], tb[s][:].indirect(idx))
+
+        ysb = [
+            keep.tile([P, N // P, R, FIRST * RU], F32, name="ysb0"),
+            keep.tile([P, N // P, R, (E - FIRST) * RU], F32, name="ysb1"),
+        ]
+        banks = {}
+        hs = {}
+
+        def first_layer(e):
+            cols = slice(e * C, (e + 1) * C)
+            pa = psum.tile([P, H], F32, name="pa")
+            pb = psum.tile([P, H], F32, name="pb")
+            for bank, words, scales in ((pa, w1, s1), (pb, w3, s3)):
+                for s in range(PASSES):
+                    nc.tensor.matmul_mx(
+                        out=bank[:],
+                        lhsT=gw[s][:, cols].bitcast(FP8X4),
+                        lhsT_scale=gb[s][:, cols],
+                        rhs=words[e][:, s, :].bitcast(FP4X4),
+                        rhs_scale=scales[:, PASSES * e + s, :],
+                        start=(s == 0),
+                        stop=(s == PASSES - 1),
+                    )
+            g = ring.tile([P, H], F32, name="g")
+            nc.scalar.activation(out=g[:], in_=pa[:], func=ACT.Gelu_apprx_tanh)
+            h = ring.tile([P, H], BF16, name="h")
+            nc.vector.tensor_tensor(
+                h[:].rearrange("p (u q d) -> p u q d", u=2, d=2),
+                pb[:].rearrange("p (q u d) -> p u q d", u=2, d=2),
+                g[:].rearrange("p (q u d) -> p u q d", u=2, d=2),
+                MULT,
+            )
+            banks[e] = h
+
+        def turn(e):
+            h = banks[e]
+            tr = psum.tile([P, 4, P], F32, name="tr")
+            for u in range(2):
+                nc.tensor.transpose(tr[:, u, :], h[:].bitcast(F32)[:, P * u : P * (u + 1)], ident[:])
+            hg = ring.tile([P, C, 4], BF16, name="hg", align_bytes=64)
+            nc.scalar.copy(out=hg[:].bitcast(F32), in_=tr[:, 0:2, :].rearrange("p u r -> p r u"))
+            hq = ring.tile([P, C], U32, name="hq", align_bytes=64)
+            hb = ring.tile([P, C], U8, name="hb", align_bytes=64)
+            nc.vector.quantize_mx(
+                out=hq[:].bitcast(FP8X4), scales=hb[:], in_=hg[:].rearrange("p c t -> p (c t)")
+            )
+            hs[e] = (hq, hb)
+
+        def second_layer(e):
+            hq, hb = hs[e]
+            y = psum.tile([P, 4, P], F32, name="y")
+            for t in range(N // P):
+                nc.tensor.matmul_mx(
+                    out=y[:, t, :],
+                    lhsT=w2[e // 3][:, e % 3, 2 * P * t : 2 * P * (t + 1)].bitcast(FP4X4),
+                    lhsT_scale=s2[:, e, P * t : P * (t + 1)],
+                    rhs=hq[:].bitcast(FP8X4),
+                    rhs_scale=hb[:],
+                    start=True,
+                    stop=True,
+                )
+            part = 0 if e < FIRST else 1
+            u0 = RU * (e - FIRST * part)
+            nc.scalar.copy(
+                out=ysb[part][:, :, :, u0 : u0 + RU], in_=y[:, 0:2, :].rearrange("p t (m u) -> p t m u", m=R)
+            )
+
+        def store(part):
+            lo = 0 if part == 0 else FIRST * RU
+            hi = FIRST * RU if part == 0 else E * RU
+            for t in range(N // P):
+                nc.sync.dma_start(
+                    out=out[P * t : P * (t + 1), :].rearrange("p (m x) -> p m x", m=R)[:, :, lo:hi],
+                    in_=ysb[part][:, t],
+                )
+
+        for step in range(E + 2):
+            if step < E:
+                first_layer(step)
+            if 1 <= step <= E:
+                turn(step - 1)
+            if step >= 2:
+                second_layer(step - 2)
+                if step - 2 == FIRST - 1:
+                    store(0)
+        store(1)

@@ -24,8 +24,8 @@ MULT = mybir.AluOpType.mult
 FLOPS = 2 * S * (2 * K * H + H * N)
 
 CHUNK = 512
-V_TOKENS = {(0, 0): 192, (0, 1): 192, (1, 0): 192, (1, 1): 320}
-GATHER = 384
+V_TOKENS = {(0, 0): 256, (0, 1): 352, (1, 0): 0, (1, 1): 384}
+GATHER = ((S,), (128, 128, 256, 256))
 FIRST = 4
 
 
@@ -35,8 +35,9 @@ def tile_moe_eps_glu_gelu_kernel(
     nc = tc.nc
     with ExitStack() as ctx:
         keep = ctx.enter_context(tc.tile_pool(name="keep", bufs=1))
-        ring = ctx.enter_context(tc.tile_pool(name="ring", bufs=2))
-        psum = ctx.enter_context(tc.psum_pool(name="psum", bufs=2))
+        stage = ctx.enter_context(tc.tile_pool(name="stage", bufs=4))
+        ring = ctx.enter_context(tc.tile_pool(name="ring", bufs=3))
+        psum = ctx.enter_context(tc.psum_pool(name="psum", bufs=3))
 
         offsets = keep.tile([P, S // 16], U16, name="offsets")
 
@@ -47,8 +48,9 @@ def tile_moe_eps_glu_gelu_kernel(
         zero = keep.tile([P, 1], F32, name="zero")
         warm = keep.tile([P, 1], F32, name="warm")
         nc.vector.memset(zero[:], 0.0)
-        for t in (s1, s3, s2):
-            nc.vector.memset(t[:].rearrange("p a b -> p (a b)").bitcast(I32), 0)
+        nc.vector.memset(s1[:].rearrange("p a b -> p (a b)").bitcast(I32), 0)
+        for t in (s3, s2):
+            nc.gpsimd.memset(t[:].rearrange("p a b -> p (a b)").bitcast(I32), 0)
         for t in tb:
             nc.vector.memset(t[:].bitcast(I32), 0)
         nc.scalar.activation(out=warm[:], in_=zero[:], func=ACT.Gelu_apprx_tanh)
@@ -58,7 +60,7 @@ def tile_moe_eps_glu_gelu_kernel(
         raw = {}
         for s in range(PASSES):
             for c in range(T // CHUNK):
-                raw[s, c] = keep.tile([P, 4, CHUNK], F32, name=f"raw{s}{c}")
+                raw[s, c] = stage.tile([P, 4, CHUNK], F32, name=f"raw{s}{c}", tag="stage", align_bytes=64)
                 nc.sync.dma_start(
                     out=raw[s, c][:],
                     in_=xT[512 * s : 512 * (s + 1), CHUNK * c : CHUNK * (c + 1)].rearrange("(p j) w -> p j w", j=4),
@@ -69,20 +71,6 @@ def tile_moe_eps_glu_gelu_kernel(
             rows = src.bitcast(I32).rearrange("e s (q r) i -> r q (e s) i", r=4)
             for r in range(4):
                 nc.sync.dma_start(out=dst[:].bitcast(I32)[r:P:32], in_=rows[r])
-        w1 = [keep.tile([P, PASSES, 2 * H], U8, name=f"w1_{e}", align_bytes=64) for e in range(E)]
-        w3 = [keep.tile([P, PASSES, 2 * H], U8, name=f"w3_{e}", align_bytes=64) for e in range(E)]
-        w2 = [keep.tile([P, E // 2, 2 * N], U8, name=f"w2_{g}", align_bytes=64) for g in range(2)]
-        for e in range(E):
-            for dst, src in ((w1, w1_words), (w3, w3_words)):
-                nc.sync.dma_start(
-                    out=dst[e][:].bitcast(I32), in_=src[e].bitcast(I32).rearrange("s p b -> p s b")
-                )
-            if e in (0, 3):
-                g = e // 3
-                nc.sync.dma_start(
-                    out=w2[g][:].bitcast(I32),
-                    in_=w2_words[3 * g : 3 * g + 3].bitcast(I32).rearrange("e s p b -> p (e s) b"),
-                )
 
         gw = [keep.tile([P, S], U32, name=f"gw{s}", align_bytes=64) for s in range(PASSES)]
         gb = [keep.tile([P, S], U8, name=f"gb{s}", align_bytes=64) for s in range(PASSES)]
@@ -90,102 +78,132 @@ def tile_moe_eps_glu_gelu_kernel(
             tw = keep.tile([P, T], U32, name=f"tw{s}", align_bytes=64)
             for c in range(T // CHUNK):
                 grouped = keep.tile([P, CHUNK, 4], BF16, name=f"grouped{s}{c}", align_bytes=64)
-                src = raw[s, c][:].rearrange("p j w -> p w j")
-                v = V_TOKENS[s, c]
-                nc.vector.tensor_copy(out=grouped[:, :v, :], in_=src[:, :v, :])
-                nc.scalar.activation(out=grouped[:, v:, :], in_=src[:, v:, :], func=ACT.Copy)
+                src = raw[s, c][:].rearrange("p j (w i) -> p w j i", i=4)
+                dst = grouped[:].rearrange("p (w i) j -> p w j i", i=4)
+                v = V_TOKENS[s, c] // 4
+                if v:
+                    nc.vector.tensor_copy(out=dst[:, :v], in_=src[:, :v])
+                nc.scalar.activation(out=dst[:, v:], in_=src[:, v:], func=ACT.Copy)
                 nc.vector.quantize_mx(
                     out=tw[:, CHUNK * c : CHUNK * (c + 1)].bitcast(FP8X4),
                     scales=tb[s][:, CHUNK * c : CHUNK * (c + 1)],
                     in_=grouped[:].rearrange("p w j -> p (w j)"),
                 )
-            for g0 in range(0, S, GATHER):
-                idx = offsets[:, g0 // 16 : (g0 + GATHER) // 16]
-                nc.vector.tensor_copy(gw[s][:, g0 : g0 + GATHER], tw[:].indirect(idx))
-                nc.vector.tensor_copy(gb[s][:, g0 : g0 + GATHER], tb[s][:].indirect(idx))
+            g0 = 0
+            for n in GATHER[s]:
+                idx = offsets[:, g0 // 16 : (g0 + n) // 16]
+                nc.vector.tensor_copy(gw[s][:, g0 : g0 + n], tw[:].indirect(idx))
+                nc.vector.tensor_copy(gb[s][:, g0 : g0 + n], tb[s][:].indirect(idx))
+                g0 = g0 + n
 
-        ysb = [
-            keep.tile([P, N // P, R, FIRST * RU], F32, name="ysb0"),
-            keep.tile([P, N // P, R, (E - FIRST) * RU], F32, name="ysb1"),
-        ]
+        w13 = []
+        for g in range(E // 2):
+            pair = stage.tile([P, 4, PASSES * 2 * H], U8, name=f"w13_{g}", tag="stage", align_bytes=64)
+            for i in range(2):
+                for m, src in enumerate((w1_words, w3_words)):
+                    nc.sync.dma_start(
+                        out=pair[:, 2 * i + m, :].bitcast(I32).rearrange("p (s b) -> p s b", s=PASSES),
+                        in_=src[2 * g + i].bitcast(I32).rearrange("s p b -> p s b"),
+                    )
+            w13.append(pair)
+        w2 = stage.tile([P, E, 2 * N], U8, name="w2", tag="stage", align_bytes=64)
+        nc.sync.dma_start(out=w2[:].bitcast(I32), in_=w2_words.bitcast(I32).rearrange("e s p b -> p (e s) b"))
+
         banks = {}
         hs = {}
+        codes = {}
 
         def first_layer(e):
             cols = slice(e * C, (e + 1) * C)
             pa = psum.tile([P, H], F32, name="pa")
             pb = psum.tile([P, H], F32, name="pb")
-            for bank, words, scales in ((pa, w1, s1), (pb, w3, s3)):
-                for s in range(PASSES):
+            for m, (bank, scales) in enumerate(((pa, s1), (pb, s3))):
+                words = w13[e // 2][:, 2 * (e % 2) + m, :]
+                for s in reversed(range(PASSES)):
                     nc.tensor.matmul_mx(
                         out=bank[:],
                         lhsT=gw[s][:, cols].bitcast(FP8X4),
                         lhsT_scale=gb[s][:, cols],
-                        rhs=words[e][:, s, :].bitcast(FP4X4),
+                        rhs=words[:, 2 * H * s : 2 * H * (s + 1)].bitcast(FP4X4),
                         rhs_scale=scales[:, PASSES * e + s, :],
-                        start=(s == 0),
-                        stop=(s == PASSES - 1),
+                        start=(s == PASSES - 1),
+                        stop=(s == 0),
                     )
             g = ring.tile([P, H], F32, name="g")
-            nc.scalar.activation(out=g[:], in_=pa[:], func=ACT.Gelu_apprx_tanh)
+            nc.scalar.activation(
+                out=g[:].rearrange("p (u q d) -> p u q d", u=2, d=2),
+                in_=pa[:].rearrange("p (q u d) -> p u q d", u=2, d=2),
+                func=ACT.Gelu_apprx_tanh,
+            )
             h = ring.tile([P, H], BF16, name="h")
             nc.vector.tensor_tensor(
                 h[:].rearrange("p (u q d) -> p u q d", u=2, d=2),
                 pb[:].rearrange("p (q u d) -> p u q d", u=2, d=2),
-                g[:].rearrange("p (q u d) -> p u q d", u=2, d=2),
+                g[:].rearrange("p (u q d) -> p u q d", u=2, d=2),
                 MULT,
             )
-            banks[e] = h
+            banks[e] = (pa, pb)
+            hs[e] = h
 
         def turn(e):
-            h = banks[e]
-            tr = psum.tile([P, 4, P], F32, name="tr")
+            h = hs[e]
+            tr = banks[e + 1][0] if e + 1 < E else banks[e][1]
             for u in range(2):
-                nc.tensor.transpose(tr[:, u, :], h[:].bitcast(F32)[:, P * u : P * (u + 1)], ident[:])
+                nc.tensor.transpose(tr[:, P * u : P * (u + 1)], h[:].bitcast(F32)[:, P * u : P * (u + 1)], ident[:])
             hg = ring.tile([P, C, 4], BF16, name="hg", align_bytes=64)
-            nc.scalar.copy(out=hg[:].bitcast(F32), in_=tr[:, 0:2, :].rearrange("p u r -> p r u"))
-            hq = ring.tile([P, C], U32, name="hq", align_bytes=64)
-            hb = ring.tile([P, C], U8, name="hb", align_bytes=64)
+            nc.scalar.copy(out=hg[:].bitcast(F32), in_=tr[:, : 2 * P].rearrange("p (u r) -> p r u", u=2))
+            hq = keep.tile([P, C], U32, name=f"hq{e}", align_bytes=64)
+            hb = keep.tile([P, C], U8, name=f"hb{e}", align_bytes=64)
             nc.vector.quantize_mx(
                 out=hq[:].bitcast(FP8X4), scales=hb[:], in_=hg[:].rearrange("p c t -> p (c t)")
             )
-            hs[e] = (hq, hb)
+            codes[e] = (hq, hb)
 
-        def second_layer(e):
-            hq, hb = hs[e]
-            y = psum.tile([P, 4, P], F32, name="y")
-            for t in range(N // P):
-                nc.tensor.matmul_mx(
-                    out=y[:, t, :],
-                    lhsT=w2[e // 3][:, e % 3, 2 * P * t : 2 * P * (t + 1)].bitcast(FP4X4),
-                    lhsT_scale=s2[:, e, P * t : P * (t + 1)],
-                    rhs=hq[:].bitcast(FP8X4),
-                    rhs_scale=hb[:],
-                    start=True,
-                    stop=True,
-                )
-            part = 0 if e < FIRST else 1
-            u0 = RU * (e - FIRST * part)
-            nc.scalar.copy(
-                out=ysb[part][:, :, :, u0 : u0 + RU], in_=y[:, 0:2, :].rearrange("p t (m u) -> p t m u", m=R)
+        def second_layer(experts, tiles, tag, bufs, copy, dst):
+            y = psum.tile([P, len(experts), len(tiles), P], F32, name="y", tag=tag, bufs=bufs)
+            for i, e in enumerate(experts):
+                hq, hb = codes[e]
+                for j, t in enumerate(tiles):
+                    nc.tensor.matmul_mx(
+                        out=y[:, i, j, :],
+                        lhsT=w2[:, e, 2 * P * t : 2 * P * (t + 1)].bitcast(FP4X4),
+                        lhsT_scale=s2[:, e, P * t : P * (t + 1)],
+                        rhs=hq[:].bitcast(FP8X4),
+                        rhs_scale=hb[:],
+                        start=True,
+                        stop=True,
+                    )
+            copy(
+                out=dst.rearrange("p t m (i u) -> p t m i u", i=len(experts)),
+                in_=y[:].rearrange("p i t (m u) -> p t m i u", m=R),
             )
 
-        def store(part):
-            lo = 0 if part == 0 else FIRST * RU
-            hi = FIRST * RU if part == 0 else E * RU
-            for t in range(N // P):
+        def store(ysb, first, tiles):
+            width = ysb.shape[3]
+            for j, t in enumerate(tiles):
                 nc.sync.dma_start(
-                    out=out[P * t : P * (t + 1), :].rearrange("p (m x) -> p m x", m=R)[:, :, lo:hi],
-                    in_=ysb[part][:, t],
+                    out=out[P * t : P * (t + 1), :].rearrange("p (m x) -> p m x", m=R)[
+                        :, :, first * RU : first * RU + width
+                    ],
+                    in_=ysb[:, j],
                 )
 
-        for step in range(E + 2):
+        for step in range(E + 1):
             if step < E:
                 first_layer(step)
-            if 1 <= step <= E:
+            if step >= 1:
                 turn(step - 1)
-            if step >= 2:
-                second_layer(step - 2)
-                if step - 2 == FIRST - 1:
-                    store(0)
-        store(1)
+        both = (0, 1)
+        y03 = keep.tile([P, 2, R, 4 * RU], F32, name="y03")
+        second_layer((0, 1), both, "y", 2, nc.scalar.copy, y03[:, :, :, : 2 * RU])
+        second_layer((2, 3), both, "y", 2, nc.vector.tensor_copy, y03[:, :, :, 2 * RU :])
+        store(y03[:], 0, both)
+        y4 = keep.tile([P, 2, R, RU], F32, name="y4")
+        second_layer((4,), both, "pb", 3, nc.scalar.copy, y4[:])
+        store(y4[:], 4, both)
+        y5a = keep.tile([P, 1, R, RU], F32, name="y5a")
+        y5b = keep.tile([P, 1, R, RU], F32, name="y5b")
+        second_layer((5,), (0,), "pa", 3, nc.scalar.copy, y5a[:])
+        second_layer((5,), (1,), "pb", 3, nc.vector.tensor_copy, y5b[:])
+        store(y5a[:], 5, (0,))
+        store(y5b[:], 5, (1,))

@@ -43,14 +43,12 @@ def tile_moe_eps_glu_gelu_kernel(
 
         s1 = keep.tile([P, E * PASSES, H], U8, name="s1", align_bytes=64)
         s3 = keep.tile([P, E * PASSES, H], U8, name="s3", align_bytes=64)
-        s2 = keep.tile([P, E, N], U8, name="s2", align_bytes=64)
         tb = [keep.tile([P, T], U8, name=f"tb{s}", align_bytes=64) for s in range(PASSES)]
         zero = keep.tile([P, 1], F32, name="zero")
         warm = keep.tile([P, 1], F32, name="warm")
         nc.vector.memset(zero[:], 0.0)
         nc.vector.memset(s1[:].rearrange("p a b -> p (a b)").bitcast(I32), 0)
-        for t in (s3, s2):
-            nc.gpsimd.memset(t[:].rearrange("p a b -> p (a b)").bitcast(I32), 0)
+        nc.gpsimd.memset(s3[:].rearrange("p a b -> p (a b)").bitcast(I32), 0)
         for t in tb:
             nc.vector.memset(t[:].bitcast(I32), 0)
         nc.scalar.activation(out=warm[:], in_=zero[:], func=ACT.Gelu_apprx_tanh)
@@ -67,10 +65,14 @@ def tile_moe_eps_glu_gelu_kernel(
                 )
                 if (s, c) == (0, 0):
                     nc.sync.dma_start(offsets[:], offs)
-        for dst, src in ((s1, w1_scales), (s3, w3_scales), (s2, w2_scales)):
+
+        def load_scales(dst, src):
             rows = src.bitcast(I32).rearrange("e s (q r) i -> r q (e s) i", r=4)
             for r in range(4):
-                nc.sync.dma_start(out=dst[:].bitcast(I32)[r:P:32], in_=rows[r])
+                nc.sync.dma_start(out=dst.bitcast(I32)[r:P:32], in_=rows[r])
+
+        load_scales(s1[:], w1_scales)
+        load_scales(s3[:], w3_scales)
 
         gw = [keep.tile([P, S], U32, name=f"gw{s}", align_bytes=64) for s in range(PASSES)]
         gb = [keep.tile([P, S], U8, name=f"gb{s}", align_bytes=64) for s in range(PASSES)]
@@ -106,8 +108,12 @@ def tile_moe_eps_glu_gelu_kernel(
                         in_=src[2 * g + i].bitcast(I32).rearrange("s p b -> p s b"),
                     )
             w13.append(pair)
-        w2 = stage.tile([P, E, 2 * N], U8, name="w2", tag="stage", align_bytes=64)
-        nc.sync.dma_start(out=w2[:].bitcast(I32), in_=w2_words.bitcast(I32).rearrange("e s p b -> p (e s) b"))
+        last = stage.tile([P, E * 3 * N], U8, name="last", tag="stage", align_bytes=64)
+        w2 = last[:, : E * 2 * N].rearrange("p (e b) -> p e b", e=E)
+        s2 = last[:, E * 2 * N :].rearrange("p (e b) -> p e b", e=E)
+        nc.vector.memset(last[:, E * 2 * N :].bitcast(I32), 0)
+        nc.sync.dma_start(out=w2.bitcast(I32), in_=w2_words.bitcast(I32).rearrange("e s p b -> p (e s) b"))
+        load_scales(s2, w2_scales)
 
         banks = {}
         hs = {}
@@ -145,19 +151,24 @@ def tile_moe_eps_glu_gelu_kernel(
             banks[e] = (pa, pb)
             hs[e] = h
 
-        def turn(e):
-            h = hs[e]
-            tr = banks[e + 1][0] if e + 1 < E else banks[e][1]
-            for u in range(2):
-                nc.tensor.transpose(tr[:, P * u : P * (u + 1)], h[:].bitcast(F32)[:, P * u : P * (u + 1)], ident[:])
-            hg = ring.tile([P, C, 4], BF16, name="hg", align_bytes=64)
-            nc.scalar.copy(out=hg[:].bitcast(F32), in_=tr[:, : 2 * P].rearrange("p (u r) -> p r u", u=2))
-            hq = keep.tile([P, C], U32, name=f"hq{e}", align_bytes=64)
-            hb = keep.tile([P, C], U8, name=f"hb{e}", align_bytes=64)
+        def turn(experts, tr):
+            n = len(experts)
+            for i, e in enumerate(experts):
+                for u in range(2):
+                    at = P * (2 * i + u)
+                    nc.tensor.transpose(tr[:, at : at + P], hs[e][:].bitcast(F32)[:, P * u : P * (u + 1)], ident[:])
+            hg = keep.tile([P, n * C, 4], BF16, name=f"hg{experts[0]}", align_bytes=64)
+            nc.scalar.copy(
+                out=hg[:].bitcast(F32).rearrange("p (i r) u -> p i r u", i=n),
+                in_=tr[:, : 2 * n * P].rearrange("p (i u r) -> p i r u", i=n, u=2),
+            )
+            hq = keep.tile([P, n * C], U32, name=f"hq{experts[0]}", align_bytes=64)
+            hb = keep.tile([P, n * C], U8, name=f"hb{experts[0]}", align_bytes=64)
             nc.vector.quantize_mx(
                 out=hq[:].bitcast(FP8X4), scales=hb[:], in_=hg[:].rearrange("p c t -> p (c t)")
             )
-            codes[e] = (hq, hb)
+            for i, e in enumerate(experts):
+                codes[e] = (hq[:, C * i : C * (i + 1)], hb[:, C * i : C * (i + 1)])
 
         def second_layer(experts, tiles, tag, bufs, copy, dst):
             y = psum.tile([P, len(experts), len(tiles), P], F32, name="y", tag=tag, bufs=bufs)
@@ -168,8 +179,8 @@ def tile_moe_eps_glu_gelu_kernel(
                         out=y[:, i, j, :],
                         lhsT=w2[:, e, 2 * P * t : 2 * P * (t + 1)].bitcast(FP4X4),
                         lhsT_scale=s2[:, e, P * t : P * (t + 1)],
-                        rhs=hq[:].bitcast(FP8X4),
-                        rhs_scale=hb[:],
+                        rhs=hq.bitcast(FP8X4),
+                        rhs_scale=hb,
                         start=True,
                         stop=True,
                     )
@@ -178,32 +189,17 @@ def tile_moe_eps_glu_gelu_kernel(
                 in_=y[:].rearrange("p i t (m u) -> p t m i u", m=R),
             )
 
-        def store(ysb, first, tiles):
-            width = ysb.shape[3]
-            for j, t in enumerate(tiles):
-                nc.sync.dma_start(
-                    out=out[P * t : P * (t + 1), :].rearrange("p (m x) -> p m x", m=R)[
-                        :, :, first * RU : first * RU + width
-                    ],
-                    in_=ysb[:, j],
-                )
 
-        for step in range(E + 1):
-            if step < E:
-                first_layer(step)
-            if step >= 1:
-                turn(step - 1)
-        both = (0, 1)
-        y03 = keep.tile([P, 2, R, 4 * RU], F32, name="y03")
-        second_layer((0, 1), both, "y", 2, nc.scalar.copy, y03[:, :, :, : 2 * RU])
-        second_layer((2, 3), both, "y", 2, nc.vector.tensor_copy, y03[:, :, :, 2 * RU :])
-        store(y03[:], 0, both)
-        y4 = keep.tile([P, 2, R, RU], F32, name="y4")
-        second_layer((4,), both, "pb", 3, nc.scalar.copy, y4[:])
-        store(y4[:], 4, both)
-        y5a = keep.tile([P, 1, R, RU], F32, name="y5a")
-        y5b = keep.tile([P, 1, R, RU], F32, name="y5b")
-        second_layer((5,), (0,), "pa", 3, nc.scalar.copy, y5a[:])
-        second_layer((5,), (1,), "pb", 3, nc.vector.tensor_copy, y5b[:])
-        store(y5a[:], 5, (0,))
-        store(y5b[:], 5, (1,))
+        for step in range(E):
+            first_layer(step)
+            if step in (2, 4):
+                turn((step - 2, step - 1), banks[step][0])
+        turn((4,), banks[5][0])
+        turn((5,), banks[5][1])
+        copies = (nc.scalar.copy, nc.vector.tensor_copy)
+        ysb = [keep.tile([P, 1, R, E * RU], F32, name=f"ysb{t}") for t in range(N // P)]
+        for t in range(N // P):
+            second_layer((0, 1, 2, 3), (t,), "y", 2, copies[t], ysb[t][:, :, :, : 4 * RU])
+        for t in range(N // P):
+            second_layer((4, 5), (t,), ("pa", "pb")[t], 3, copies[t], ysb[t][:, :, :, 4 * RU :])
+            nc.sync.dma_start(out=out[P * t : P * (t + 1), :], in_=ysb[t][:].rearrange("p t m x -> p (t m x)"))

@@ -25,7 +25,6 @@ FLOPS = 2 * S * (2 * K * H + H * N)
 
 CHUNK = 512
 V_TOKENS = {(0, 0): 256, (0, 1): 352, (1, 0): 0, (1, 1): 384}
-GATHER = ((S,), (128, 128, 256, 256))
 FIRST = 4
 
 
@@ -37,6 +36,7 @@ def tile_moe_eps_glu_gelu_kernel(
         keep = ctx.enter_context(tc.tile_pool(name="keep", bufs=1))
         stage = ctx.enter_context(tc.tile_pool(name="stage", bufs=4))
         ring = ctx.enter_context(tc.tile_pool(name="ring", bufs=3))
+        lay = ctx.enter_context(tc.tile_pool(name="lay", bufs=1))
         psum = ctx.enter_context(tc.psum_pool(name="psum", bufs=3))
 
         offsets = keep.tile([P, S // 16], U16, name="offsets")
@@ -71,15 +71,42 @@ def tile_moe_eps_glu_gelu_kernel(
             for r in range(4):
                 nc.sync.dma_start(out=dst.bitcast(I32)[r:P:32], in_=rows[r])
 
+        w13 = {}
+
+        def load_weights(slot, m, first, count):
+            src = (w1_words, w3_words)[m][first : first + count]
+            rows = slot[:, 2 * m + first % 2 : 2 * m + first % 2 + count, :]
+            nc.sync.dma_start(
+                out=rows.bitcast(I32).rearrange("p e (s b) -> p (e s) b", s=PASSES),
+                in_=src.bitcast(I32).rearrange("e s p b -> p (e s) b"),
+            )
+            for i in range(count):
+                w13[first + i, m] = rows[:, i, :]
+
+        head = keep.tile([P, 4, PASSES * 2 * H], U8, name="head", align_bytes=64)
+        load_weights(head, 0, 0, 2)
+        load_weights(head, 1, 0, 2)
         load_scales(s1[:], w1_scales)
         load_scales(s3[:], w3_scales)
 
-        gw = [keep.tile([P, S], U32, name=f"gw{s}", align_bytes=64) for s in range(PASSES)]
-        gb = [keep.tile([P, S], U8, name=f"gb{s}", align_bytes=64) for s in range(PASSES)]
+        tw = [keep.tile([P, T], U32, name=f"tw{s}", align_bytes=64) for s in range(PASSES)]
+        tokens = {}
+
+        def gather(s, experts, words, scales):
+            idx = offsets[:, experts[0] * C // 16 : (experts[-1] + 1) * C // 16]
+            nc.vector.tensor_copy(words, tw[s][:].indirect(idx))
+            nc.vector.tensor_copy(scales, tb[s][:].indirect(idx))
+            for i, e in enumerate(experts):
+                tokens[e, s] = (words[:, C * i : C * (i + 1)], scales[:, C * i : C * (i + 1)])
+
+        gw = keep.tile([P, PASSES, 4 * C], U32, name="gw", align_bytes=64)
+        gb = keep.tile([P, PASSES, 4 * C], U8, name="gb", align_bytes=64)
         for s in range(PASSES):
-            tw = keep.tile([P, T], U32, name=f"tw{s}", align_bytes=64)
             for c in range(T // CHUNK):
-                grouped = keep.tile([P, CHUNK, 4], BF16, name=f"grouped{s}{c}", align_bytes=64)
+                if (s, c) == (1, 1):
+                    grouped = lay.tile([P, CHUNK, 4], BF16, name="grouped11", align_bytes=64, offset=0)
+                else:
+                    grouped = keep.tile([P, CHUNK, 4], BF16, name=f"grouped{s}{c}", align_bytes=64)
                 src = raw[s, c][:].rearrange("p j (w i) -> p w j i", i=4)
                 dst = grouped[:].rearrange("p (w i) j -> p w j i", i=4)
                 v = V_TOKENS[s, c] // 4
@@ -87,27 +114,26 @@ def tile_moe_eps_glu_gelu_kernel(
                     nc.vector.tensor_copy(out=dst[:, :v], in_=src[:, :v])
                 nc.scalar.activation(out=dst[:, v:], in_=src[:, v:], func=ACT.Copy)
                 nc.vector.quantize_mx(
-                    out=tw[:, CHUNK * c : CHUNK * (c + 1)].bitcast(FP8X4),
+                    out=tw[s][:, CHUNK * c : CHUNK * (c + 1)].bitcast(FP8X4),
                     scales=tb[s][:, CHUNK * c : CHUNK * (c + 1)],
                     in_=grouped[:].rearrange("p w j -> p (w j)"),
                 )
-            g0 = 0
-            for n in GATHER[s]:
-                idx = offsets[:, g0 // 16 : (g0 + n) // 16]
-                nc.vector.tensor_copy(gw[s][:, g0 : g0 + n], tw[:].indirect(idx))
-                nc.vector.tensor_copy(gb[s][:, g0 : g0 + n], tb[s][:].indirect(idx))
-                g0 = g0 + n
+            if s == 0:
+                gather(0, (0, 1, 2, 3), gw[:, 0, :], gb[:, 0, :])
+        gather(1, (0,), gw[:, 1, :C], gb[:, 1, :C])
+        gather(1, (1,), gw[:, 1, C : 2 * C], gb[:, 1, C : 2 * C])
+        gather(1, (2, 3), gw[:, 1, 2 * C :], gb[:, 1, 2 * C :])
+        gw0 = lay.tile([P, 2 * C], U32, name="gw0", align_bytes=64, offset=0)
+        gb0 = lay.tile([P, 2 * C], U8, name="gb0", align_bytes=64, offset=1024)
+        gather(0, (4, 5), gw0[:], gb0[:])
 
-        w13 = []
-        for g in range(E // 2):
-            pair = stage.tile([P, 4, PASSES * 2 * H], U8, name=f"w13_{g}", tag="stage", align_bytes=64)
-            for i in range(2):
-                for m, src in enumerate((w1_words, w3_words)):
-                    nc.sync.dma_start(
-                        out=pair[:, 2 * i + m, :].bitcast(I32).rearrange("p (s b) -> p s b", s=PASSES),
-                        in_=src[2 * g + i].bitcast(I32).rearrange("s p b -> p s b"),
-                    )
-            w13.append(pair)
+        slot = stage.tile([P, 4, PASSES * 2 * H], U8, name="w13_23", tag="stage", align_bytes=64)
+        load_weights(slot, 0, 2, 2)
+        load_weights(slot, 1, 2, 2)
+        slot = stage.tile([P, 4, PASSES * 2 * H], U8, name="w13_45", tag="stage", align_bytes=64)
+        load_weights(slot, 0, 4, 2)
+        load_weights(slot, 1, 4, 1)
+        load_weights(slot, 1, 5, 1)
         last = stage.tile([P, E * 3 * N], U8, name="last", tag="stage", align_bytes=64)
         w2 = last[:, : E * 2 * N].rearrange("p (e b) -> p e b", e=E)
         s2 = last[:, E * 2 * N :].rearrange("p (e b) -> p e b", e=E)
@@ -120,22 +146,24 @@ def tile_moe_eps_glu_gelu_kernel(
         codes = {}
 
         def first_layer(e):
-            cols = slice(e * C, (e + 1) * C)
             pa = psum.tile([P, H], F32, name="pa")
             pb = psum.tile([P, H], F32, name="pb")
             for m, (bank, scales) in enumerate(((pa, s1), (pb, s3))):
-                words = w13[e // 2][:, 2 * (e % 2) + m, :]
+                words = w13[e, m]
                 for s in reversed(range(PASSES)):
                     nc.tensor.matmul_mx(
                         out=bank[:],
-                        lhsT=gw[s][:, cols].bitcast(FP8X4),
-                        lhsT_scale=gb[s][:, cols],
+                        lhsT=tokens[e, s][0].bitcast(FP8X4),
+                        lhsT_scale=tokens[e, s][1],
                         rhs=words[:, 2 * H * s : 2 * H * (s + 1)].bitcast(FP4X4),
                         rhs_scale=scales[:, PASSES * e + s, :],
                         start=(s == PASSES - 1),
                         stop=(s == 0),
                     )
-            g = ring.tile([P, H], F32, name="g")
+            if e == 1:
+                g = lay.tile([P, H], F32, name="g_first", align_bytes=64, offset=4096)
+            else:
+                g = ring.tile([P, H], F32, name="g")
             nc.scalar.activation(
                 out=g[:].rearrange("p (u q d) -> p u q d", u=2, d=2),
                 in_=pa[:].rearrange("p (q u d) -> p u q d", u=2, d=2),
@@ -192,6 +220,10 @@ def tile_moe_eps_glu_gelu_kernel(
 
         for step in range(E):
             first_layer(step)
+            if step == 1:
+                gw1 = lay.tile([P, 2 * C], U32, name="gw1", align_bytes=64, offset=4096)
+                gb1 = lay.tile([P, 2 * C], U8, name="gb1", align_bytes=64, offset=4096 + 1024)
+                gather(1, (4, 5), gw1[:], gb1[:])
             if step in (2, 4):
                 turn((step - 2, step - 1), banks[step][0])
         turn((4,), banks[5][0])

@@ -24,8 +24,7 @@ MULT = mybir.AluOpType.mult
 FLOPS = 2 * S * (2 * K * H + H * N)
 
 CHUNK = 512
-V_TOKENS = {(0, 0): 256, (0, 1): 352, (1, 0): 0, (1, 1): 384}
-FIRST = 4
+V_TOKENS = (672, 512)
 
 
 def tile_moe_eps_glu_gelu_kernel(
@@ -34,7 +33,7 @@ def tile_moe_eps_glu_gelu_kernel(
     nc = tc.nc
     with ExitStack() as ctx:
         keep = ctx.enter_context(tc.tile_pool(name="keep", bufs=1))
-        stage = ctx.enter_context(tc.tile_pool(name="stage", bufs=4))
+        stage = ctx.enter_context(tc.tile_pool(name="stage", bufs=2))
         ring = ctx.enter_context(tc.tile_pool(name="ring", bufs=3))
         lay = ctx.enter_context(tc.tile_pool(name="lay", bufs=1))
         psum = ctx.enter_context(tc.psum_pool(name="psum", bufs=3))
@@ -55,16 +54,13 @@ def tile_moe_eps_glu_gelu_kernel(
         ident = keep.tile([P, P], F32, name="ident")
         make_identity(nc, ident[:])
 
-        raw = {}
+        raw = []
         for s in range(PASSES):
-            for c in range(T // CHUNK):
-                raw[s, c] = stage.tile([P, 4, CHUNK], F32, name=f"raw{s}{c}", tag="stage", align_bytes=64)
-                nc.sync.dma_start(
-                    out=raw[s, c][:],
-                    in_=xT[512 * s : 512 * (s + 1), CHUNK * c : CHUNK * (c + 1)].rearrange("(p j) w -> p j w", j=4),
-                )
-                if (s, c) == (0, 0):
-                    nc.sync.dma_start(offsets[:], offs)
+            rows = stage.tile([P, 4, T], F32, name=f"raw{s}", tag="stage", align_bytes=64)
+            nc.sync.dma_start(out=rows[:], in_=xT[512 * s : 512 * (s + 1), :].rearrange("(p j) w -> p j w", j=4))
+            raw.append(rows)
+            if s == 0:
+                nc.sync.dma_start(offsets[:], offs)
 
         def load_scales(dst, src):
             rows = src.bitcast(I32).rearrange("e s (q r) i -> r q (e s) i", r=4)
@@ -102,17 +98,21 @@ def tile_moe_eps_glu_gelu_kernel(
         gw = keep.tile([P, PASSES, 4 * C], U32, name="gw", align_bytes=64)
         gb = keep.tile([P, PASSES, 4 * C], U8, name="gb", align_bytes=64)
         for s in range(PASSES):
+            halves = []
             for c in range(T // CHUNK):
                 if (s, c) == (1, 1):
                     grouped = lay.tile([P, CHUNK, 4], BF16, name="grouped11", align_bytes=64, offset=0)
                 else:
                     grouped = keep.tile([P, CHUNK, 4], BF16, name=f"grouped{s}{c}", align_bytes=64)
-                src = raw[s, c][:].rearrange("p j (w i) -> p w j i", i=4)
+                src = raw[s][:, :, CHUNK * c : CHUNK * (c + 1)].rearrange("p j (w i) -> p w j i", i=4)
                 dst = grouped[:].rearrange("p (w i) j -> p w j i", i=4)
-                v = V_TOKENS[s, c] // 4
+                v = min(V_TOKENS[s] - CHUNK * c, CHUNK) // 4
                 if v:
                     nc.vector.tensor_copy(out=dst[:, :v], in_=src[:, :v])
-                nc.scalar.activation(out=dst[:, v:], in_=src[:, v:], func=ACT.Copy)
+                if 4 * v < CHUNK:
+                    nc.scalar.activation(out=dst[:, v:], in_=src[:, v:], func=ACT.Copy)
+                halves.append(grouped)
+            for c, grouped in enumerate(halves):
                 nc.vector.quantize_mx(
                     out=tw[s][:, CHUNK * c : CHUNK * (c + 1)].bitcast(FP8X4),
                     scales=tb[s][:, CHUNK * c : CHUNK * (c + 1)],
@@ -127,13 +127,18 @@ def tile_moe_eps_glu_gelu_kernel(
         gb0 = lay.tile([P, 2 * C], U8, name="gb0", align_bytes=64, offset=1024)
         gather(0, (4, 5), gw0[:], gb0[:])
 
-        slot = stage.tile([P, 4, PASSES * 2 * H], U8, name="w13_23", tag="stage", align_bytes=64)
+        rest = stage.tile([P, 2, 4, PASSES * 2 * H], U8, name="rest", tag="stage", align_bytes=64)
+        slot = rest[:, 0]
         load_weights(slot, 0, 2, 2)
         load_weights(slot, 1, 2, 2)
-        slot = stage.tile([P, 4, PASSES * 2 * H], U8, name="w13_45", tag="stage", align_bytes=64)
+        slot = rest[:, 1]
         load_weights(slot, 0, 4, 2)
         load_weights(slot, 1, 4, 1)
-        load_weights(slot, 1, 5, 1)
+        w13[5, 1] = slot[:, 3, :]
+        for s in reversed(range(PASSES)):
+            nc.sync.dma_start(
+                out=w13[5, 1][:, 2 * H * s : 2 * H * (s + 1)].bitcast(I32), in_=w3_words[5, s].bitcast(I32)
+            )
         last = stage.tile([P, E * 3 * N], U8, name="last", tag="stage", align_bytes=64)
         w2 = last[:, : E * 2 * N].rearrange("p (e b) -> p e b", e=E)
         s2 = last[:, E * 2 * N :].rearrange("p (e b) -> p e b", e=E)

@@ -24,7 +24,8 @@ MULT = mybir.AluOpType.mult
 FLOPS = 2 * S * (2 * K * H + H * N)
 
 CHUNK = 512
-V_TOKENS = (672, 512)
+V_HALF = 344
+V_PASS1 = 512
 
 
 def tile_moe_eps_glu_gelu_kernel(
@@ -33,159 +34,151 @@ def tile_moe_eps_glu_gelu_kernel(
     nc = tc.nc
     with ExitStack() as ctx:
         keep = ctx.enter_context(tc.tile_pool(name="keep", bufs=1))
-        stage = ctx.enter_context(tc.tile_pool(name="stage", bufs=2))
-        ring = ctx.enter_context(tc.tile_pool(name="ring", bufs=3))
+        ring = ctx.enter_context(tc.tile_pool(name="ring", bufs=E))
         lay = ctx.enter_context(tc.tile_pool(name="lay", bufs=1))
-        psum = ctx.enter_context(tc.psum_pool(name="psum", bufs=3))
+        psum = ctx.enter_context(tc.psum_pool(name="psum", bufs=8))
 
         offsets = keep.tile([P, S // 16], U16, name="offsets")
 
-        s1 = keep.tile([P, E * PASSES, H], U8, name="s1", align_bytes=64)
-        s3 = keep.tile([P, E * PASSES, H], U8, name="s3", align_bytes=64)
         tb = [keep.tile([P, T], U8, name=f"tb{s}", align_bytes=64) for s in range(PASSES)]
         zero = keep.tile([P, 1], F32, name="zero")
         warm = keep.tile([P, 1], F32, name="warm")
         nc.vector.memset(zero[:], 0.0)
-        nc.vector.memset(s1[:].rearrange("p a b -> p (a b)").bitcast(I32), 0)
-        nc.gpsimd.memset(s3[:].rearrange("p a b -> p (a b)").bitcast(I32), 0)
         for t in tb:
             nc.vector.memset(t[:].bitcast(I32), 0)
         nc.scalar.activation(out=warm[:], in_=zero[:], func=ACT.Gelu_apprx_tanh)
         ident = keep.tile([P, P], F32, name="ident")
         make_identity(nc, ident[:])
 
-        raw = []
-        for s in range(PASSES):
-            rows = stage.tile([P, 4, T], F32, name=f"raw{s}", tag="stage", align_bytes=64)
-            nc.sync.dma_start(out=rows[:], in_=xT[512 * s : 512 * (s + 1), :].rearrange("(p j) w -> p j w", j=4))
-            raw.append(rows)
-            if s == 0:
-                nc.sync.dma_start(offsets[:], offs)
+        half_bytes = 4 * CHUNK * 4
+        raw0 = []
+        for c in range(T // CHUNK):
+            rows = lay.tile([P, 4, CHUNK], F32, name=f"raw0{c}", align_bytes=64, offset=half_bytes * c)
+            nc.sync.dma_start(
+                out=rows[:], in_=xT[:512, CHUNK * c : CHUNK * (c + 1)].rearrange("(p j) w -> p j w", j=4)
+            )
+            raw0.append(rows)
+        nc.sync.dma_start(offsets[:], offs)
+        raw1 = keep.tile([P, 4, T], F32, name="raw1", align_bytes=64)
+        nc.sync.dma_start(out=raw1[:], in_=xT[512:, :].rearrange("(p j) w -> p j w", j=4))
+
+        def round_tokens(src, dst, v):
+            src = src.rearrange("p j (w i) -> p w j i", i=4)
+            dst = dst.rearrange("p (w i) j -> p w j i", i=4)
+            if v:
+                nc.vector.tensor_copy(out=dst[:, : v // 4], in_=src[:, : v // 4])
+            if v < CHUNK:
+                nc.scalar.activation(out=dst[:, v // 4 :], in_=src[:, v // 4 :], func=ACT.Copy)
+
+        tw = [keep.tile([P, T], U32, name=f"tw{s}", align_bytes=64) for s in range(PASSES)]
+        gw = keep.tile([P, PASSES, S], U32, name="gw", align_bytes=64)
+        gb = keep.tile([P, PASSES, S], U8, name="gb", align_bytes=64)
+
+        def quantise(s, c, grouped):
+            cols = slice(CHUNK * c, CHUNK * (c + 1))
+            nc.vector.quantize_mx(
+                out=tw[s][:, cols].bitcast(FP8X4),
+                scales=tb[s][:, cols],
+                in_=grouped[:, cols, :].rearrange("p w j -> p (w j)"),
+            )
+
+        def gather(s, first, count):
+            idx = offsets[:, first * C // 16 : (first + count) * C // 16]
+            cols = slice(first * C, (first + count) * C)
+            nc.vector.tensor_copy(gw[:, s, cols], tw[s][:].indirect(idx))
+            nc.vector.tensor_copy(gb[:, s, cols], tb[s][:].indirect(idx))
+
+        grouped = keep.tile([P, T, 4], BF16, name="grouped0", tag="grouped", align_bytes=64)
+        for c in range(T // CHUNK):
+            round_tokens(raw0[c][:], grouped[:, CHUNK * c : CHUNK * (c + 1), :], V_HALF)
+            quantise(0, c, grouped)
+        gather(0, 0, E)
+        grouped = keep.tile([P, T, 4], BF16, name="grouped1", tag="grouped", align_bytes=64)
+        for c in range(T // CHUNK):
+            cols = slice(CHUNK * c, CHUNK * (c + 1))
+            round_tokens(raw1[:, :, cols], grouped[:, cols, :], min(V_PASS1 - CHUNK * c, CHUNK))
+        for c in range(T // CHUNK):
+            quantise(1, c, grouped)
+        for first in range(0, E, 2):
+            gather(1, first, 2)
 
         def load_scales(dst, src):
             rows = src.bitcast(I32).rearrange("e s (q r) i -> r q (e s) i", r=4)
             for r in range(4):
                 nc.sync.dma_start(out=dst.bitcast(I32)[r:P:32], in_=rows[r])
 
-        w13 = {}
+        plane = E * PASSES * H
+        s1 = lay.tile([P, E * PASSES, H], U8, name="s1", align_bytes=64, offset=0)
+        s3 = lay.tile([P, E * PASSES, H], U8, name="s3", align_bytes=64, offset=plane)
+        s2 = lay.tile([P, E, N], U8, name="s2", align_bytes=64, offset=2 * plane)
+        w = lay.tile([P, 2 * E * PASSES * 2 * H + E * 2 * N], U8, name="w", align_bytes=64, offset=2 * plane + E * N)
+        w13 = w[:, : 2 * E * PASSES * 2 * H].rearrange("p (m e s b) -> p m e s b", m=2, e=E, s=PASSES)
+        w2 = w[:, 2 * E * PASSES * 2 * H :].rearrange("p (e b) -> p e b", e=E)
 
-        def load_weights(slot, m, first, count):
+        def load_weights(m, first, count):
             src = (w1_words, w3_words)[m][first : first + count]
-            rows = slot[:, 2 * m + first % 2 : 2 * m + first % 2 + count, :]
             nc.sync.dma_start(
-                out=rows.bitcast(I32).rearrange("p e (s b) -> p (e s) b", s=PASSES),
+                out=w13[:, m, first : first + count].bitcast(I32).rearrange("p e s b -> p (e s) b"),
                 in_=src.bitcast(I32).rearrange("e s p b -> p (e s) b"),
             )
-            for i in range(count):
-                w13[first + i, m] = rows[:, i, :]
 
-        head = keep.tile([P, 4, PASSES * 2 * H], U8, name="head", align_bytes=64)
-        load_weights(head, 0, 0, 2)
-        load_weights(head, 1, 0, 2)
         load_scales(s1[:], w1_scales)
+        load_weights(0, 0, 2)
+        load_weights(0, 2, 2)
         load_scales(s3[:], w3_scales)
-
-        tw = [keep.tile([P, T], U32, name=f"tw{s}", align_bytes=64) for s in range(PASSES)]
-        tokens = {}
-
-        def gather(s, experts, words, scales):
-            idx = offsets[:, experts[0] * C // 16 : (experts[-1] + 1) * C // 16]
-            nc.vector.tensor_copy(words, tw[s][:].indirect(idx))
-            nc.vector.tensor_copy(scales, tb[s][:].indirect(idx))
-            for i, e in enumerate(experts):
-                tokens[e, s] = (words[:, C * i : C * (i + 1)], scales[:, C * i : C * (i + 1)])
-
-        gw = keep.tile([P, PASSES, 4 * C], U32, name="gw", align_bytes=64)
-        gb = keep.tile([P, PASSES, 4 * C], U8, name="gb", align_bytes=64)
-        for s in range(PASSES):
-            halves = []
-            for c in range(T // CHUNK):
-                if (s, c) == (1, 1):
-                    grouped = lay.tile([P, CHUNK, 4], BF16, name="grouped11", align_bytes=64, offset=0)
-                else:
-                    grouped = keep.tile([P, CHUNK, 4], BF16, name=f"grouped{s}{c}", align_bytes=64)
-                src = raw[s][:, :, CHUNK * c : CHUNK * (c + 1)].rearrange("p j (w i) -> p w j i", i=4)
-                dst = grouped[:].rearrange("p (w i) j -> p w j i", i=4)
-                v = min(V_TOKENS[s] - CHUNK * c, CHUNK) // 4
-                if v:
-                    nc.vector.tensor_copy(out=dst[:, :v], in_=src[:, :v])
-                if 4 * v < CHUNK:
-                    nc.scalar.activation(out=dst[:, v:], in_=src[:, v:], func=ACT.Copy)
-                halves.append(grouped)
-            for c, grouped in enumerate(halves):
-                nc.vector.quantize_mx(
-                    out=tw[s][:, CHUNK * c : CHUNK * (c + 1)].bitcast(FP8X4),
-                    scales=tb[s][:, CHUNK * c : CHUNK * (c + 1)],
-                    in_=grouped[:].rearrange("p w j -> p (w j)"),
-                )
-            if s == 0:
-                gather(0, (0, 1, 2, 3), gw[:, 0, :], gb[:, 0, :])
-        gather(1, (0,), gw[:, 1, :C], gb[:, 1, :C])
-        gather(1, (1,), gw[:, 1, C : 2 * C], gb[:, 1, C : 2 * C])
-        gather(1, (2, 3), gw[:, 1, 2 * C :], gb[:, 1, 2 * C :])
-        gw0 = lay.tile([P, 2 * C], U32, name="gw0", align_bytes=64, offset=0)
-        gb0 = lay.tile([P, 2 * C], U8, name="gb0", align_bytes=64, offset=1024)
-        gather(0, (4, 5), gw0[:], gb0[:])
-
-        rest = stage.tile([P, 2, 4, PASSES * 2 * H], U8, name="rest", tag="stage", align_bytes=64)
-        slot = rest[:, 0]
-        load_weights(slot, 0, 2, 2)
-        load_weights(slot, 1, 2, 2)
-        slot = rest[:, 1]
-        load_weights(slot, 0, 4, 2)
-        load_weights(slot, 1, 4, 1)
-        w13[5, 1] = slot[:, 3, :]
+        for e in range(4):
+            load_weights(1, e, 1)
+        load_weights(0, 4, 1)
+        load_weights(1, 4, 1)
+        load_weights(0, 5, 1)
         for s in reversed(range(PASSES)):
-            nc.sync.dma_start(
-                out=w13[5, 1][:, 2 * H * s : 2 * H * (s + 1)].bitcast(I32), in_=w3_words[5, s].bitcast(I32)
-            )
-        last = stage.tile([P, E * 3 * N], U8, name="last", tag="stage", align_bytes=64)
-        w2 = last[:, : E * 2 * N].rearrange("p (e b) -> p e b", e=E)
-        s2 = last[:, E * 2 * N :].rearrange("p (e b) -> p e b", e=E)
-        nc.vector.memset(last[:, E * 2 * N :].bitcast(I32), 0)
+            nc.sync.dma_start(out=w13[:, 1, 5, s, :].bitcast(I32), in_=w3_words[5, s].bitcast(I32))
         nc.sync.dma_start(out=w2.bitcast(I32), in_=w2_words.bitcast(I32).rearrange("e s p b -> p (e s) b"))
-        load_scales(s2, w2_scales)
+        load_scales(s2[:], w2_scales)
 
         banks = {}
+        gs = {}
         hs = {}
         codes = {}
 
-        def first_layer(e):
-            pa = psum.tile([P, H], F32, name="pa")
-            pb = psum.tile([P, H], F32, name="pb")
-            for m, (bank, scales) in enumerate(((pa, s1), (pb, s3))):
-                words = w13[e, m]
-                for s in reversed(range(PASSES)):
-                    nc.tensor.matmul_mx(
-                        out=bank[:],
-                        lhsT=tokens[e, s][0].bitcast(FP8X4),
-                        lhsT_scale=tokens[e, s][1],
-                        rhs=words[:, 2 * H * s : 2 * H * (s + 1)].bitcast(FP4X4),
-                        rhs_scale=scales[:, PASSES * e + s, :],
-                        start=(s == PASSES - 1),
-                        stop=(s == 0),
-                    )
-            if e == 1:
-                g = lay.tile([P, H], F32, name="g_first", align_bytes=64, offset=4096)
-            else:
-                g = ring.tile([P, H], F32, name="g")
+        def product(bank, m, e, s, start):
+            cols = slice(C * e, C * (e + 1))
+            nc.tensor.matmul_mx(
+                out=bank[:],
+                lhsT=gw[:, s, cols].bitcast(FP8X4),
+                lhsT_scale=gb[:, s, cols],
+                rhs=w13[:, m, e, s, :].bitcast(FP4X4),
+                rhs_scale=(s1, s3)[m][:, PASSES * e + s, :],
+                start=start,
+                stop=not start,
+            )
+
+        def gate(e):
+            g = ring.tile([P, H], F32, name="g")
             nc.scalar.activation(
                 out=g[:].rearrange("p (u q d) -> p u q d", u=2, d=2),
-                in_=pa[:].rearrange("p (q u d) -> p u q d", u=2, d=2),
+                in_=banks[e, 0][:].rearrange("p (q u d) -> p u q d", u=2, d=2),
                 func=ACT.Gelu_apprx_tanh,
             )
+            gs[e] = g
+
+        def hidden(e):
+            pb = psum.tile([P, H], F32, name="pb", tag="bank")
+            banks[e, 1] = pb
+            product(pb, 1, e, 1, True)
+            product(pb, 1, e, 0, False)
             h = ring.tile([P, H], BF16, name="h")
             nc.vector.tensor_tensor(
                 h[:].rearrange("p (u q d) -> p u q d", u=2, d=2),
                 pb[:].rearrange("p (q u d) -> p u q d", u=2, d=2),
-                g[:].rearrange("p (u q d) -> p u q d", u=2, d=2),
+                gs[e][:].rearrange("p (u q d) -> p u q d", u=2, d=2),
                 MULT,
             )
-            banks[e] = (pa, pb)
             hs[e] = h
 
-        def turn(experts, tr):
+        def turn(experts):
             n = len(experts)
+            tr = psum.tile([P, H], F32, name="tr", tag="bank")
             for i, e in enumerate(experts):
                 for u in range(2):
                     at = P * (2 * i + u)
@@ -203,8 +196,8 @@ def tile_moe_eps_glu_gelu_kernel(
             for i, e in enumerate(experts):
                 codes[e] = (hq[:, C * i : C * (i + 1)], hb[:, C * i : C * (i + 1)])
 
-        def second_layer(experts, tiles, tag, bufs, copy, dst):
-            y = psum.tile([P, len(experts), len(tiles), P], F32, name="y", tag=tag, bufs=bufs)
+        def second_layer(experts, tiles, copy, dst):
+            y = psum.tile([P, len(experts), len(tiles), P], F32, name="y", tag="bank")
             for i, e in enumerate(experts):
                 hq, hb = codes[e]
                 for j, t in enumerate(tiles):
@@ -222,21 +215,32 @@ def tile_moe_eps_glu_gelu_kernel(
                 in_=y[:].rearrange("p i t (m u) -> p t m i u", m=R),
             )
 
+        def gated(e):
+            banks[e, 0] = psum.tile([P, H], F32, name="pa", tag="bank")
+            product(banks[e, 0], 0, e, 1, True)
+            product(banks[e, 0], 0, e, 0, False)
+            gate(e)
 
-        for step in range(E):
-            first_layer(step)
-            if step == 1:
-                gw1 = lay.tile([P, 2 * C], U32, name="gw1", align_bytes=64, offset=4096)
-                gb1 = lay.tile([P, 2 * C], U8, name="gb1", align_bytes=64, offset=4096 + 1024)
-                gather(1, (4, 5), gw1[:], gb1[:])
-            if step in (2, 4):
-                turn((step - 2, step - 1), banks[step][0])
-        turn((4,), banks[5][0])
-        turn((5,), banks[5][1])
+        for e in range(4):
+            banks[e, 0] = psum.tile([P, H], F32, name="pa", tag="bank")
+            product(banks[e, 0], 0, e, 0, True)
+        for e in range(4):
+            product(banks[e, 0], 0, e, 1, False)
+            gate(e)
+        for e in range(4):
+            hidden(e)
+        turn((0, 1))
+        gated(4)
+        hidden(4)
+        gated(5)
+        hidden(5)
+        turn((2, 3))
+        turn((4,))
+        turn((5,))
         copies = (nc.scalar.copy, nc.vector.tensor_copy)
         ysb = [keep.tile([P, 1, R, E * RU], F32, name=f"ysb{t}") for t in range(N // P)]
         for t in range(N // P):
-            second_layer((0, 1, 2, 3), (t,), "y", 2, copies[t], ysb[t][:, :, :, : 4 * RU])
+            second_layer((0, 1, 2, 3), (t,), copies[t], ysb[t][:, :, :, : 4 * RU])
         for t in range(N // P):
-            second_layer((4, 5), (t,), ("pa", "pb")[t], 3, copies[t], ysb[t][:, :, :, 4 * RU :])
+            second_layer((4, 5), (t,), copies[t], ysb[t][:, :, :, 4 * RU :])
             nc.sync.dma_start(out=out[P * t : P * (t + 1), :], in_=ysb[t][:].rearrange("p t m x -> p (t m x)"))

@@ -25,7 +25,9 @@ FLOPS = 2 * S * (2 * K * H + H * N)
 
 CHUNK = 512
 V_HALF = 344
-V_PASS1 = 512
+V_PASS1 = 96
+HEAD = 2
+WARM = 3
 
 
 def tile_moe_eps_glu_gelu_kernel(
@@ -59,8 +61,27 @@ def tile_moe_eps_glu_gelu_kernel(
             )
             raw0.append(rows)
         nc.sync.dma_start(offsets[:], offs)
-        raw1 = keep.tile([P, 4, T], F32, name="raw1", align_bytes=64)
-        nc.sync.dma_start(out=raw1[:], in_=xT[512:, :].rearrange("(p j) w -> p j w", j=4))
+        raw1 = []
+        for c in range(T // CHUNK):
+            rows = keep.tile([P, 4, CHUNK], F32, name=f"raw1{c}", align_bytes=64)
+            nc.sync.dma_start(
+                out=rows[:], in_=xT[512:, CHUNK * c : CHUNK * (c + 1)].rearrange("(p j) w -> p j w", j=4)
+            )
+            raw1.append(rows)
+        weights = {}
+
+        def load_weights(dst, m, first):
+            count = dst.shape[1]
+            src = (w1_words, w3_words)[m][first : first + count]
+            nc.sync.dma_start(
+                out=dst.bitcast(I32).rearrange("p e s b -> p (e s) b"),
+                in_=src.bitcast(I32).rearrange("e s p b -> p (e s) b"),
+            )
+            for i in range(count):
+                weights[m, first + i] = dst[:, i]
+
+        head = keep.tile([P, HEAD, PASSES, 2 * H], U8, name="head", align_bytes=64)
+        load_weights(head[:], 0, 0)
 
         def round_tokens(src, dst, v):
             src = src.rearrange("p j (w i) -> p w j i", i=4)
@@ -96,45 +117,40 @@ def tile_moe_eps_glu_gelu_kernel(
         grouped = keep.tile([P, T, 4], BF16, name="grouped1", tag="grouped", align_bytes=64)
         for c in range(T // CHUNK):
             cols = slice(CHUNK * c, CHUNK * (c + 1))
-            round_tokens(raw1[:, :, cols], grouped[:, cols, :], min(V_PASS1 - CHUNK * c, CHUNK))
+            round_tokens(raw1[c][:], grouped[:, cols, :], V_PASS1 * c)
         for c in range(T // CHUNK):
             quantise(1, c, grouped)
         for first in range(0, E, 2):
             gather(1, first, 2)
 
-        def load_scales(dst, src):
+        def load_scales(dst, src, halved):
             rows = src.bitcast(I32).rearrange("e s (q r) i -> r q (e s) i", r=4)
             for r in range(4):
-                nc.sync.dma_start(out=dst.bitcast(I32)[r:P:32], in_=rows[r])
+                parts = 2 if r >= 4 - halved else 1
+                n = dst.shape[1] // parts
+                for part in range(parts):
+                    at = slice(n * part, n * (part + 1))
+                    nc.sync.dma_start(out=dst.bitcast(I32)[r:P:32, at], in_=rows[r][:, at])
 
         plane = E * PASSES * H
         s1 = lay.tile([P, E * PASSES, H], U8, name="s1", align_bytes=64, offset=0)
         s3 = lay.tile([P, E * PASSES, H], U8, name="s3", align_bytes=64, offset=plane)
         s2 = lay.tile([P, E, N], U8, name="s2", align_bytes=64, offset=2 * plane)
-        w = lay.tile([P, 2 * E * PASSES * 2 * H + E * 2 * N], U8, name="w", align_bytes=64, offset=2 * plane + E * N)
-        w13 = w[:, : 2 * E * PASSES * 2 * H].rearrange("p (m e s b) -> p m e s b", m=2, e=E, s=PASSES)
-        w2 = w[:, 2 * E * PASSES * 2 * H :].rearrange("p (e b) -> p e b", e=E)
+        later = [(1, e) for e in range(HEAD)] + [(m, e) for e in range(HEAD, E) for m in range(2)]
+        matrix = PASSES * 2 * H
+        w = lay.tile([P, len(later) * matrix + E * 2 * N], U8, name="w", align_bytes=64, offset=2 * plane + E * N)
+        w13 = w[:, : len(later) * matrix].rearrange("p (a s b) -> p a s b", s=PASSES, b=2 * H)
+        w2 = w[:, len(later) * matrix : len(later) * matrix + E * 2 * N].rearrange("p (e b) -> p e b", e=E)
 
-        def load_weights(m, first, count):
-            src = (w1_words, w3_words)[m][first : first + count]
-            nc.sync.dma_start(
-                out=w13[:, m, first : first + count].bitcast(I32).rearrange("p e s b -> p (e s) b"),
-                in_=src.bitcast(I32).rearrange("e s p b -> p (e s) b"),
-            )
-
-        load_scales(s1[:], w1_scales)
-        load_weights(0, 0, 2)
-        load_weights(0, 2, 2)
-        load_scales(s3[:], w3_scales)
-        for e in range(4):
-            load_weights(1, e, 1)
-        load_weights(0, 4, 1)
-        load_weights(1, 4, 1)
-        load_weights(0, 5, 1)
+        load_scales(s1[:], w1_scales, 0)
+        load_scales(s3[:], w3_scales, 2)
+        for a, (m, e) in enumerate(later[:-1]):
+            load_weights(w13[:, a : a + 1], m, e)
+        weights[later[-1]] = w13[:, len(later) - 1]
         for s in reversed(range(PASSES)):
-            nc.sync.dma_start(out=w13[:, 1, 5, s, :].bitcast(I32), in_=w3_words[5, s].bitcast(I32))
+            nc.sync.dma_start(out=weights[1, E - 1][:, s, :].bitcast(I32), in_=w3_words[E - 1, s].bitcast(I32))
         nc.sync.dma_start(out=w2.bitcast(I32), in_=w2_words.bitcast(I32).rearrange("e s p b -> p (e s) b"))
-        load_scales(s2[:], w2_scales)
+        load_scales(s2[:], w2_scales, 0)
 
         banks = {}
         gs = {}
@@ -147,7 +163,7 @@ def tile_moe_eps_glu_gelu_kernel(
                 out=bank[:],
                 lhsT=gw[:, s, cols].bitcast(FP8X4),
                 lhsT_scale=gb[:, s, cols],
-                rhs=w13[:, m, e, s, :].bitcast(FP4X4),
+                rhs=weights[m, e][:, s, :].bitcast(FP4X4),
                 rhs_scale=(s1, s3)[m][:, PASSES * e + s, :],
                 start=start,
                 stop=not start,
@@ -221,19 +237,29 @@ def tile_moe_eps_glu_gelu_kernel(
             product(banks[e, 0], 0, e, 0, False)
             gate(e)
 
-        for e in range(4):
+        for e in range(HEAD):
             banks[e, 0] = psum.tile([P, H], F32, name="pa", tag="bank")
+        for i in range(WARM):
+            nc.tensor.matmul_mx(
+                out=banks[0, 0][:],
+                lhsT=gw[:, 0, :C].bitcast(FP8X4),
+                lhsT_scale=gb[:, 0, :C],
+                rhs=weights[0, 0][:, 0, :].bitcast(FP4X4),
+                rhs_scale=gb[:, 0, :H],
+                start=True,
+                stop=True,
+            )
+        for e in range(HEAD):
             product(banks[e, 0], 0, e, 0, True)
-        for e in range(4):
+        for e in range(HEAD):
             product(banks[e, 0], 0, e, 1, False)
             gate(e)
-        for e in range(4):
+        for e in range(E):
+            if e >= HEAD:
+                gated(e)
             hidden(e)
-        turn((0, 1))
-        gated(4)
-        hidden(4)
-        gated(5)
-        hidden(5)
+            if e == 3:
+                turn((0, 1))
         turn((2, 3))
         turn((4,))
         turn((5,))

@@ -24,8 +24,7 @@ MULT = mybir.AluOpType.mult
 FLOPS = 2 * S * (2 * K * H + H * N)
 
 CHUNK = 512
-V_HALF = 344
-V_PASS1 = 96
+V_SHARE = ((344, 232), (136, 240))
 HEAD = 2
 WARM = 3
 
@@ -52,22 +51,11 @@ def tile_moe_eps_glu_gelu_kernel(
         ident = keep.tile([P, P], F32, name="ident")
         make_identity(nc, ident[:])
 
-        half_bytes = 4 * CHUNK * 4
-        raw0 = []
-        for c in range(T // CHUNK):
-            rows = lay.tile([P, 4, CHUNK], F32, name=f"raw0{c}", align_bytes=64, offset=half_bytes * c)
-            nc.sync.dma_start(
-                out=rows[:], in_=xT[:512, CHUNK * c : CHUNK * (c + 1)].rearrange("(p j) w -> p j w", j=4)
-            )
-            raw0.append(rows)
+        raw0 = lay.tile([P, 4, T], F32, name="raw0", align_bytes=64, offset=0)
+        nc.sync.dma_start(out=raw0[:], in_=xT[:512, :].rearrange("(p j) w -> p j w", j=4))
         nc.sync.dma_start(offsets[:], offs)
-        raw1 = []
-        for c in range(T // CHUNK):
-            rows = keep.tile([P, 4, CHUNK], F32, name=f"raw1{c}", align_bytes=64)
-            nc.sync.dma_start(
-                out=rows[:], in_=xT[512:, CHUNK * c : CHUNK * (c + 1)].rearrange("(p j) w -> p j w", j=4)
-            )
-            raw1.append(rows)
+        raw1 = keep.tile([P, 4, T], F32, name="raw1", align_bytes=64)
+        nc.sync.dma_start(out=raw1[:], in_=xT[512:, :].rearrange("(p j) w -> p j w", j=4))
         weights = {}
 
         def load_weights(dst, m, first):
@@ -100,7 +88,7 @@ def tile_moe_eps_glu_gelu_kernel(
             nc.vector.quantize_mx(
                 out=tw[s][:, cols].bitcast(FP8X4),
                 scales=tb[s][:, cols],
-                in_=grouped[:, cols, :].rearrange("p w j -> p (w j)"),
+                in_=grouped[:].rearrange("p w j -> p (w j)"),
             )
 
         def gather(s, first, count):
@@ -109,17 +97,13 @@ def tile_moe_eps_glu_gelu_kernel(
             nc.vector.tensor_copy(gw[:, s, cols], tw[s][:].indirect(idx))
             nc.vector.tensor_copy(gb[:, s, cols], tb[s][:].indirect(idx))
 
-        grouped = keep.tile([P, T, 4], BF16, name="grouped0", tag="grouped", align_bytes=64)
-        for c in range(T // CHUNK):
-            round_tokens(raw0[c][:], grouped[:, CHUNK * c : CHUNK * (c + 1), :], V_HALF)
-            quantise(0, c, grouped)
-        gather(0, 0, E)
-        grouped = keep.tile([P, T, 4], BF16, name="grouped1", tag="grouped", align_bytes=64)
-        for c in range(T // CHUNK):
-            cols = slice(CHUNK * c, CHUNK * (c + 1))
-            round_tokens(raw1[c][:], grouped[:, cols, :], V_PASS1 * c)
-        for c in range(T // CHUNK):
-            quantise(1, c, grouped)
+        for s, raw in enumerate((raw0, raw1)):
+            for c in range(T // CHUNK):
+                grouped = keep.tile([P, CHUNK, 4], BF16, name=f"grouped{s}{c}", tag=f"grouped{c}", align_bytes=64)
+                round_tokens(raw[:, :, CHUNK * c : CHUNK * (c + 1)], grouped[:], V_SHARE[s][c])
+                quantise(s, c, grouped)
+            if s == 0:
+                gather(0, 0, E)
         for first in range(0, E, 2):
             gather(1, first, 2)
 

@@ -7,7 +7,8 @@ K, T, E, C, H, N = 1024, 1024, 6, 128, 512, 256
 R = 4
 S = E * C
 P = 128
-PASSES = K // 512
+K_PASS = 4 * P
+PASSES = K // K_PASS
 RU = C // R
 
 F32 = mybir.dt.float32
@@ -23,10 +24,14 @@ MULT = mybir.AluOpType.mult
 
 FLOPS = 2 * S * (2 * K * H + H * N)
 
-CHUNK = 512
+HALF = T // 2
 V_SHARE = ((344, 232), (136, 240))
 HEAD = 2
+EARLY = 4
 WARM = 3
+BANKS = 8
+MX_ALIGN = 64
+DMA_ALIGN = 256
 
 
 def tile_moe_eps_glu_gelu_kernel(
@@ -37,25 +42,26 @@ def tile_moe_eps_glu_gelu_kernel(
         keep = ctx.enter_context(tc.tile_pool(name="keep", bufs=1))
         ring = ctx.enter_context(tc.tile_pool(name="ring", bufs=E))
         lay = ctx.enter_context(tc.tile_pool(name="lay", bufs=1))
-        psum = ctx.enter_context(tc.psum_pool(name="psum", bufs=8))
+        psum = ctx.enter_context(tc.psum_pool(name="psum", bufs=BANKS))
 
         offsets = keep.tile([P, S // 16], U16, name="offsets")
 
-        tb = [keep.tile([P, T], U8, name=f"tb{s}", align_bytes=64) for s in range(PASSES)]
+        token_scales = [keep.tile([P, T], U8, name=f"token_scales{s}", align_bytes=MX_ALIGN) for s in range(PASSES)]
         zero = keep.tile([P, 1], F32, name="zero")
         warm = keep.tile([P, 1], F32, name="warm")
         nc.vector.memset(zero[:], 0.0)
-        for t in tb:
-            nc.vector.memset(t[:].bitcast(I32), 0)
+        for tile in token_scales:
+            nc.vector.memset(tile[:].bitcast(I32), 0)
         nc.scalar.activation(out=warm[:], in_=zero[:], func=ACT.Gelu_apprx_tanh)
         ident = keep.tile([P, P], F32, name="ident")
         make_identity(nc, ident[:])
 
-        raw0 = lay.tile([P, 4, T], F32, name="raw0", align_bytes=64, offset=0)
-        nc.sync.dma_start(out=raw0[:], in_=xT[:512, :].rearrange("(p j) w -> p j w", j=4))
+        raw0 = lay.tile([P, 4, T], F32, name="raw0", align_bytes=DMA_ALIGN, offset=0)
+        nc.sync.dma_start(out=raw0[:], in_=xT[:K_PASS, :].rearrange("(p j) w -> p j w", j=4))
         nc.sync.dma_start(offsets[:], offs)
-        raw1 = keep.tile([P, 4, T], F32, name="raw1", align_bytes=64)
-        nc.sync.dma_start(out=raw1[:], in_=xT[512:, :].rearrange("(p j) w -> p j w", j=4))
+        raw1 = keep.tile([P, 4, T], F32, name="raw1", align_bytes=DMA_ALIGN)
+        nc.sync.dma_start(out=raw1[:], in_=xT[K_PASS:, :].rearrange("(p j) w -> p j w", j=4))
+
         weights = {}
 
         def load_weights(dst, m, first):
@@ -68,39 +74,37 @@ def tile_moe_eps_glu_gelu_kernel(
             for i in range(count):
                 weights[m, first + i] = dst[:, i]
 
-        head = keep.tile([P, HEAD, PASSES, 2 * H], U8, name="head", align_bytes=64)
+        head = keep.tile([P, HEAD, PASSES, 2 * H], U8, name="head", align_bytes=DMA_ALIGN)
         load_weights(head[:], 0, 0)
 
-        def round_tokens(src, dst, v):
+        def round_tokens(src, dst, share):
             src = src.rearrange("p j (w i) -> p w j i", i=4)
             dst = dst.rearrange("p (w i) j -> p w j i", i=4)
-            if v:
-                nc.vector.tensor_copy(out=dst[:, : v // 4], in_=src[:, : v // 4])
-            if v < CHUNK:
-                nc.scalar.activation(out=dst[:, v // 4 :], in_=src[:, v // 4 :], func=ACT.Copy)
+            nc.vector.tensor_copy(out=dst[:, : share // 4], in_=src[:, : share // 4])
+            nc.scalar.activation(out=dst[:, share // 4 :], in_=src[:, share // 4 :], func=ACT.Copy)
 
-        tw = [keep.tile([P, T], U32, name=f"tw{s}", align_bytes=64) for s in range(PASSES)]
-        gw = keep.tile([P, PASSES, S], U32, name="gw", align_bytes=64)
-        gb = keep.tile([P, PASSES, S], U8, name="gb", align_bytes=64)
+        token_words = [keep.tile([P, T], U32, name=f"token_words{s}", align_bytes=MX_ALIGN) for s in range(PASSES)]
+        slot_words = keep.tile([P, PASSES, S], U32, name="slot_words", align_bytes=MX_ALIGN)
+        slot_scales = keep.tile([P, PASSES, S], U8, name="slot_scales", align_bytes=MX_ALIGN)
 
         def quantise(s, c, grouped):
-            cols = slice(CHUNK * c, CHUNK * (c + 1))
+            cols = slice(HALF * c, HALF * (c + 1))
             nc.vector.quantize_mx(
-                out=tw[s][:, cols].bitcast(FP8X4),
-                scales=tb[s][:, cols],
+                out=token_words[s][:, cols].bitcast(FP8X4),
+                scales=token_scales[s][:, cols],
                 in_=grouped[:].rearrange("p w j -> p (w j)"),
             )
 
         def gather(s, first, count):
             idx = offsets[:, first * C // 16 : (first + count) * C // 16]
             cols = slice(first * C, (first + count) * C)
-            nc.vector.tensor_copy(gw[:, s, cols], tw[s][:].indirect(idx))
-            nc.vector.tensor_copy(gb[:, s, cols], tb[s][:].indirect(idx))
+            nc.vector.tensor_copy(slot_words[:, s, cols], token_words[s][:].indirect(idx))
+            nc.vector.tensor_copy(slot_scales[:, s, cols], token_scales[s][:].indirect(idx))
 
         for s, raw in enumerate((raw0, raw1)):
-            for c in range(T // CHUNK):
-                grouped = keep.tile([P, CHUNK, 4], BF16, name=f"grouped{s}{c}", tag=f"grouped{c}", align_bytes=64)
-                round_tokens(raw[:, :, CHUNK * c : CHUNK * (c + 1)], grouped[:], V_SHARE[s][c])
+            for c in range(T // HALF):
+                grouped = keep.tile([P, HALF, 4], BF16, name=f"grouped{s}{c}", tag=f"grouped{c}", align_bytes=MX_ALIGN)
+                round_tokens(raw[:, :, HALF * c : HALF * (c + 1)], grouped[:], V_SHARE[s][c])
                 quantise(s, c, grouped)
             if s == 0:
                 gather(0, 0, E)
@@ -111,20 +115,21 @@ def tile_moe_eps_glu_gelu_kernel(
             rows = src.bitcast(I32).rearrange("e s (q r) i -> r q (e s) i", r=4)
             for r in range(4):
                 parts = 2 if r >= 4 - halved else 1
-                n = dst.shape[1] // parts
+                width = dst.shape[1] // parts
                 for part in range(parts):
-                    at = slice(n * part, n * (part + 1))
+                    at = slice(width * part, width * (part + 1))
                     nc.sync.dma_start(out=dst.bitcast(I32)[r:P:32, at], in_=rows[r][:, at])
 
-        plane = E * PASSES * H
-        s1 = lay.tile([P, E * PASSES, H], U8, name="s1", align_bytes=64, offset=0)
-        s3 = lay.tile([P, E * PASSES, H], U8, name="s3", align_bytes=64, offset=plane)
-        s2 = lay.tile([P, E, N], U8, name="s2", align_bytes=64, offset=2 * plane)
+        scale_bytes = E * PASSES * H
+        s1 = lay.tile([P, E * PASSES, H], U8, name="s1", align_bytes=DMA_ALIGN, offset=0)
+        s3 = lay.tile([P, E * PASSES, H], U8, name="s3", align_bytes=DMA_ALIGN, offset=scale_bytes)
+        s2 = lay.tile([P, E, N], U8, name="s2", align_bytes=DMA_ALIGN, offset=2 * scale_bytes)
         later = [(1, e) for e in range(HEAD)] + [(m, e) for e in range(HEAD, E) for m in range(2)]
-        matrix = PASSES * 2 * H
-        w = lay.tile([P, len(later) * matrix + E * 2 * N], U8, name="w", align_bytes=64, offset=2 * plane + E * N)
-        w13 = w[:, : len(later) * matrix].rearrange("p (a s b) -> p a s b", s=PASSES, b=2 * H)
-        w2 = w[:, len(later) * matrix : len(later) * matrix + E * 2 * N].rearrange("p (e b) -> p e b", e=E)
+        matrix_bytes = PASSES * 2 * H
+        w13_bytes = len(later) * matrix_bytes
+        w = lay.tile([P, w13_bytes + E * 2 * N], U8, name="w", align_bytes=DMA_ALIGN, offset=2 * scale_bytes + E * N)
+        w13 = w[:, :w13_bytes].rearrange("p (a s b) -> p a s b", s=PASSES, b=2 * H)
+        w2 = w[:, w13_bytes:].rearrange("p (e b) -> p e b", e=E)
 
         load_scales(s1[:], w1_scales, 0)
         load_scales(s3[:], w3_scales, 2)
@@ -136,17 +141,17 @@ def tile_moe_eps_glu_gelu_kernel(
         nc.sync.dma_start(out=w2.bitcast(I32), in_=w2_words.bitcast(I32).rearrange("e s p b -> p (e s) b"))
         load_scales(s2[:], w2_scales, 0)
 
-        banks = {}
-        gs = {}
+        a_banks = {}
+        gelus = {}
         hs = {}
-        codes = {}
+        h_codes = {}
 
         def product(bank, m, e, s, start):
             cols = slice(C * e, C * (e + 1))
             nc.tensor.matmul_mx(
                 out=bank[:],
-                lhsT=gw[:, s, cols].bitcast(FP8X4),
-                lhsT_scale=gb[:, s, cols],
+                lhsT=slot_words[:, s, cols].bitcast(FP8X4),
+                lhsT_scale=slot_scales[:, s, cols],
                 rhs=weights[m, e][:, s, :].bitcast(FP4X4),
                 rhs_scale=(s1, s3)[m][:, PASSES * e + s, :],
                 start=start,
@@ -157,100 +162,97 @@ def tile_moe_eps_glu_gelu_kernel(
             g = ring.tile([P, H], F32, name="g")
             nc.scalar.activation(
                 out=g[:].rearrange("p (u q d) -> p u q d", u=2, d=2),
-                in_=banks[e, 0][:].rearrange("p (q u d) -> p u q d", u=2, d=2),
+                in_=a_banks[e][:].rearrange("p (q u d) -> p u q d", u=2, d=2),
                 func=ACT.Gelu_apprx_tanh,
             )
-            gs[e] = g
+            gelus[e] = g
 
         def hidden(e):
-            pb = psum.tile([P, H], F32, name="pb", tag="bank")
-            banks[e, 1] = pb
-            product(pb, 1, e, 1, True)
-            product(pb, 1, e, 0, False)
+            b = psum.tile([P, H], F32, name="b", tag="bank")
+            product(b, 1, e, 1, True)
+            product(b, 1, e, 0, False)
             h = ring.tile([P, H], BF16, name="h")
             nc.vector.tensor_tensor(
                 h[:].rearrange("p (u q d) -> p u q d", u=2, d=2),
-                pb[:].rearrange("p (q u d) -> p u q d", u=2, d=2),
-                gs[e][:].rearrange("p (u q d) -> p u q d", u=2, d=2),
+                b[:].rearrange("p (q u d) -> p u q d", u=2, d=2),
+                gelus[e][:].rearrange("p (u q d) -> p u q d", u=2, d=2),
                 MULT,
             )
             hs[e] = h
 
         def turn(experts):
-            n = len(experts)
-            tr = psum.tile([P, H], F32, name="tr", tag="bank")
+            count = len(experts)
+            turned = psum.tile([P, H], F32, name="turned", tag="bank")
             for i, e in enumerate(experts):
                 for u in range(2):
                     at = P * (2 * i + u)
-                    nc.tensor.transpose(tr[:, at : at + P], hs[e][:].bitcast(F32)[:, P * u : P * (u + 1)], ident[:])
-            hg = keep.tile([P, n * C, 4], BF16, name=f"hg{experts[0]}", align_bytes=64)
+                    words = hs[e][:].bitcast(F32)[:, P * u : P * (u + 1)]
+                    nc.tensor.transpose(turned[:, at : at + P], words, ident[:])
+            h_grouped = keep.tile([P, count * C, 4], BF16, name=f"h_grouped{experts[0]}", align_bytes=MX_ALIGN)
             nc.scalar.copy(
-                out=hg[:].bitcast(F32).rearrange("p (i r) u -> p i r u", i=n),
-                in_=tr[:, : 2 * n * P].rearrange("p (i u r) -> p i r u", i=n, u=2),
+                out=h_grouped[:].bitcast(F32).rearrange("p (i r) u -> p i r u", i=count),
+                in_=turned[:, : 2 * count * P].rearrange("p (i u r) -> p i r u", i=count, u=2),
             )
-            hq = keep.tile([P, n * C], U32, name=f"hq{experts[0]}", align_bytes=64)
-            hb = keep.tile([P, n * C], U8, name=f"hb{experts[0]}", align_bytes=64)
+            h_words = keep.tile([P, count * C], U32, name=f"h_words{experts[0]}", align_bytes=MX_ALIGN)
+            h_scales = keep.tile([P, count * C], U8, name=f"h_scales{experts[0]}", align_bytes=MX_ALIGN)
             nc.vector.quantize_mx(
-                out=hq[:].bitcast(FP8X4), scales=hb[:], in_=hg[:].rearrange("p c t -> p (c t)")
+                out=h_words[:].bitcast(FP8X4), scales=h_scales[:], in_=h_grouped[:].rearrange("p c t -> p (c t)")
             )
             for i, e in enumerate(experts):
-                codes[e] = (hq[:, C * i : C * (i + 1)], hb[:, C * i : C * (i + 1)])
+                h_codes[e] = (h_words[:, C * i : C * (i + 1)], h_scales[:, C * i : C * (i + 1)])
 
-        def second_layer(experts, tiles, copy, dst):
-            y = psum.tile([P, len(experts), len(tiles), P], F32, name="y", tag="bank")
+        def second_layer(experts, t, copy, dst):
+            y = psum.tile([P, len(experts), C], F32, name="y", tag="bank")
             for i, e in enumerate(experts):
-                hq, hb = codes[e]
-                for j, t in enumerate(tiles):
-                    nc.tensor.matmul_mx(
-                        out=y[:, i, j, :],
-                        lhsT=w2[:, e, 2 * P * t : 2 * P * (t + 1)].bitcast(FP4X4),
-                        lhsT_scale=s2[:, e, P * t : P * (t + 1)],
-                        rhs=hq.bitcast(FP8X4),
-                        rhs_scale=hb,
-                        start=True,
-                        stop=True,
-                    )
+                h_words, h_scales = h_codes[e]
+                nc.tensor.matmul_mx(
+                    out=y[:, i, :],
+                    lhsT=w2[:, e, 2 * P * t : 2 * P * (t + 1)].bitcast(FP4X4),
+                    lhsT_scale=s2[:, e, P * t : P * (t + 1)],
+                    rhs=h_words.bitcast(FP8X4),
+                    rhs_scale=h_scales,
+                    start=True,
+                    stop=True,
+                )
             copy(
-                out=dst.rearrange("p t m (i u) -> p t m i u", i=len(experts)),
-                in_=y[:].rearrange("p i t (m u) -> p t m i u", m=R),
+                out=dst.rearrange("p m (i u) -> p m i u", i=len(experts)),
+                in_=y[:].rearrange("p i (m u) -> p m i u", m=R),
             )
-
-        def gated(e):
-            banks[e, 0] = psum.tile([P, H], F32, name="pa", tag="bank")
-            product(banks[e, 0], 0, e, 1, True)
-            product(banks[e, 0], 0, e, 0, False)
-            gate(e)
 
         for e in range(HEAD):
-            banks[e, 0] = psum.tile([P, H], F32, name="pa", tag="bank")
+            a_banks[e] = psum.tile([P, H], F32, name="a", tag="bank")
         for i in range(WARM):
             nc.tensor.matmul_mx(
-                out=banks[0, 0][:],
-                lhsT=gw[:, 0, :C].bitcast(FP8X4),
-                lhsT_scale=gb[:, 0, :C],
+                out=a_banks[0][:],
+                lhsT=slot_words[:, 0, :C].bitcast(FP8X4),
+                lhsT_scale=slot_scales[:, 0, :C],
                 rhs=weights[0, 0][:, 0, :].bitcast(FP4X4),
-                rhs_scale=gb[:, 0, :H],
+                rhs_scale=slot_scales[:, 0, :H],
                 start=True,
                 stop=True,
             )
         for e in range(HEAD):
-            product(banks[e, 0], 0, e, 0, True)
+            product(a_banks[e], 0, e, 0, True)
         for e in range(HEAD):
-            product(banks[e, 0], 0, e, 1, False)
+            product(a_banks[e], 0, e, 1, False)
             gate(e)
         for e in range(E):
             if e >= HEAD:
-                gated(e)
+                a_banks[e] = psum.tile([P, H], F32, name="a", tag="bank")
+                product(a_banks[e], 0, e, 1, True)
+                product(a_banks[e], 0, e, 0, False)
+                gate(e)
             hidden(e)
-            if e == 3:
+            if e == EARLY - 1:
                 turn((0, 1))
         turn((2, 3))
-        turn((4,))
-        turn((5,))
+        for e in range(EARLY, E):
+            turn((e,))
+
         copies = (nc.scalar.copy, nc.vector.tensor_copy)
-        ysb = [keep.tile([P, 1, R, E * RU], F32, name=f"ysb{t}") for t in range(N // P)]
+        results = [keep.tile([P, R, E * RU], F32, name=f"results{t}", align_bytes=DMA_ALIGN) for t in range(N // P)]
         for t in range(N // P):
-            second_layer((0, 1, 2, 3), (t,), copies[t], ysb[t][:, :, :, : 4 * RU])
+            second_layer(range(EARLY), t, copies[t], results[t][:, :, : EARLY * RU])
         for t in range(N // P):
-            second_layer((4, 5), (t,), copies[t], ysb[t][:, :, :, 4 * RU :])
-            nc.sync.dma_start(out=out[P * t : P * (t + 1), :], in_=ysb[t][:].rearrange("p t m x -> p (t m x)"))
+            second_layer(range(EARLY, E), t, copies[t], results[t][:, :, EARLY * RU :])
+            nc.sync.dma_start(out=out[P * t : P * (t + 1), :], in_=results[t][:].rearrange("p m x -> p (m x)"))

@@ -26,9 +26,9 @@ FLOPS = 2 * S * (2 * K * H + H * N)
 
 HALF = T // 2
 V_SHARE = ((344, 232), (136, 240))
-HEAD = 2
+HEAD = 4
 EARLY = 4
-WARM = 3
+WARM = (512, 512, 256)
 BANKS = 8
 MX_ALIGN = 64
 DMA_ALIGN = 256
@@ -221,13 +221,13 @@ def tile_moe_eps_glu_gelu_kernel(
 
         for e in range(HEAD):
             a_banks[e] = psum.tile([P, H], F32, name="a", tag="bank")
-        for i in range(WARM):
+        for width in WARM:
             nc.tensor.matmul_mx(
-                out=a_banks[0][:],
+                out=a_banks[0][:, :width],
                 lhsT=slot_words[:, 0, :C].bitcast(FP8X4),
                 lhsT_scale=slot_scales[:, 0, :C],
-                rhs=weights[0, 0][:, 0, :].bitcast(FP4X4),
-                rhs_scale=slot_scales[:, 0, :H],
+                rhs=weights[0, 0][:, 0, : 2 * width].bitcast(FP4X4),
+                rhs_scale=slot_scales[:, 0, :width],
                 start=True,
                 stop=True,
             )

@@ -25,8 +25,8 @@ MULT = mybir.AluOpType.mult
 FLOPS = 2 * S * (2 * K * H + H * N)
 
 HALF = T // 2
-V_SHARE = ((344, 232), (136, 240))
-HEAD = 4
+V_SHARE = ((232, 376), (0, 304))
+HEAD = 2
 EARLY = 4
 WARM = (512, 512, 256)
 BANKS = 8
@@ -80,7 +80,8 @@ def tile_moe_eps_glu_gelu_kernel(
         def round_tokens(src, dst, share):
             src = src.rearrange("p j (w i) -> p w j i", i=4)
             dst = dst.rearrange("p (w i) j -> p w j i", i=4)
-            nc.vector.tensor_copy(out=dst[:, : share // 4], in_=src[:, : share // 4])
+            if share:
+                nc.vector.tensor_copy(out=dst[:, : share // 4], in_=src[:, : share // 4])
             nc.scalar.activation(out=dst[:, share // 4 :], in_=src[:, share // 4 :], func=ACT.Copy)
 
         token_words = [keep.tile([P, T], U32, name=f"token_words{s}", align_bytes=MX_ALIGN) for s in range(PASSES)]
@@ -102,9 +103,12 @@ def tile_moe_eps_glu_gelu_kernel(
             nc.vector.tensor_copy(slot_scales[:, s, cols], token_scales[s][:].indirect(idx))
 
         for s, raw in enumerate((raw0, raw1)):
+            halves = []
             for c in range(T // HALF):
                 grouped = keep.tile([P, HALF, 4], BF16, name=f"grouped{s}{c}", tag=f"grouped{c}", align_bytes=MX_ALIGN)
                 round_tokens(raw[:, :, HALF * c : HALF * (c + 1)], grouped[:], V_SHARE[s][c])
+                halves.append(grouped)
+            for c, grouped in enumerate(halves):
                 quantise(s, c, grouped)
             if s == 0:
                 gather(0, 0, E)

@@ -128,7 +128,8 @@ def tile_moe_eps_glu_gelu_kernel(
         s1 = lay.tile([P, E * PASSES, H], U8, name="s1", align_bytes=DMA_ALIGN, offset=0)
         s3 = lay.tile([P, E * PASSES, H], U8, name="s3", align_bytes=DMA_ALIGN, offset=scale_bytes)
         s2 = lay.tile([P, E, N], U8, name="s2", align_bytes=DMA_ALIGN, offset=2 * scale_bytes)
-        later = [(1, e) for e in range(HEAD)] + [(m, e) for e in range(HEAD, E) for m in range(2)]
+        later = [(1, e) for e in range(HEAD)] + [(m, e) for e in range(HEAD, E - 2) for m in range(2)]
+        later = later + [(m, e) for m in range(2) for e in range(E - 2, E)]
         matrix_bytes = PASSES * 2 * H
         w13_bytes = len(later) * matrix_bytes
         w = lay.tile([P, w13_bytes + E * 2 * N], U8, name="w", align_bytes=DMA_ALIGN, offset=2 * scale_bytes + E * N)
@@ -184,7 +185,7 @@ def tile_moe_eps_glu_gelu_kernel(
             )
             hs[e] = h
 
-        def turn(experts):
+        def turn(experts, copy):
             count = len(experts)
             turned = psum.tile([P, H], F32, name="turned", tag="bank")
             for i, e in enumerate(experts):
@@ -193,7 +194,7 @@ def tile_moe_eps_glu_gelu_kernel(
                     words = hs[e][:].bitcast(F32)[:, P * u : P * (u + 1)]
                     nc.tensor.transpose(turned[:, at : at + P], words, ident[:])
             h_grouped = keep.tile([P, count * C, 4], BF16, name=f"h_grouped{experts[0]}", align_bytes=MX_ALIGN)
-            nc.scalar.copy(
+            copy(
                 out=h_grouped[:].bitcast(F32).rearrange("p (i r) u -> p i r u", i=count),
                 in_=turned[:, : 2 * count * P].rearrange("p (i u r) -> p i r u", i=count, u=2),
             )
@@ -205,8 +206,8 @@ def tile_moe_eps_glu_gelu_kernel(
             for i, e in enumerate(experts):
                 h_codes[e] = (h_words[:, C * i : C * (i + 1)], h_scales[:, C * i : C * (i + 1)])
 
-        def second_layer(experts, t, copy, dst):
-            y = psum.tile([P, len(experts), C], F32, name="y", tag="bank")
+        def second_layer(experts, t, bank, copy, dst):
+            y = bank[:, : len(experts) * C].rearrange("p (i c) -> p i c", c=C)
             for i, e in enumerate(experts):
                 h_words, h_scales = h_codes[e]
                 nc.tensor.matmul_mx(
@@ -220,7 +221,7 @@ def tile_moe_eps_glu_gelu_kernel(
                 )
             copy(
                 out=dst.rearrange("p m (i u) -> p m i u", i=len(experts)),
-                in_=y[:].rearrange("p i (m u) -> p m i u", m=R),
+                in_=y.rearrange("p i (m u) -> p m i u", m=R),
             )
 
         for e in range(HEAD):
@@ -240,23 +241,29 @@ def tile_moe_eps_glu_gelu_kernel(
         for e in range(HEAD):
             product(a_banks[e], 0, e, 1, False)
             gate(e)
-        for e in range(E):
-            if e >= HEAD:
+        scalar_copy, vector_copy = nc.scalar.copy, nc.vector.tensor_copy
+        for m, e in later:
+            if m == 0:
                 a_banks[e] = psum.tile([P, H], F32, name="a", tag="bank")
                 product(a_banks[e], 0, e, 1, True)
                 product(a_banks[e], 0, e, 0, False)
                 gate(e)
-            hidden(e)
-            if e == EARLY - 1:
-                turn((0, 1))
-        turn((2, 3))
-        for e in range(EARLY, E):
-            turn((e,))
+            else:
+                hidden(e)
+        turn((0, 1), scalar_copy)
+        turn((2,), vector_copy)
+        turn((3, 4), scalar_copy)
+        turn((5,), scalar_copy)
 
-        copies = (nc.scalar.copy, nc.vector.tensor_copy)
-        results = [keep.tile([P, R, E * RU], F32, name=f"results{t}", align_bytes=DMA_ALIGN) for t in range(N // P)]
+        def fresh():
+            return psum.tile([P, H], F32, name="y", tag="bank")
+
+        parts = (
+            (((0, 1, 2), scalar_copy), ((3, 4), scalar_copy), ((5,), vector_copy)),
+            (((0, 1, 2), vector_copy), ((3, 4, 5), scalar_copy)),
+        )
         for t in range(N // P):
-            second_layer(range(EARLY), t, copies[t], results[t][:, :, : EARLY * RU])
-        for t in range(N // P):
-            second_layer(range(EARLY, E), t, copies[t], results[t][:, :, EARLY * RU :])
-            nc.sync.dma_start(out=out[P * t : P * (t + 1), :], in_=results[t][:].rearrange("p m x -> p (m x)"))
+            result = keep.tile([P, R, E * RU], F32, name=f"result{t}", align_bytes=DMA_ALIGN)
+            for experts, copy in parts[t]:
+                second_layer(experts, t, fresh(), copy, result[:, :, experts[0] * RU : (experts[-1] + 1) * RU])
+            nc.sync.dma_start(out=out[P * t : P * (t + 1), :], in_=result[:].rearrange("p m x -> p (m x)"))

@@ -25,7 +25,8 @@ MULT = mybir.AluOpType.mult
 FLOPS = 2 * S * (2 * K * H + H * N)
 
 HALF = T // 2
-V_SHARE = ((232, 376), (0, 304))
+V_SHARE = ((232, 376), (160, 392))
+LATE = 4
 HEAD = 2
 EARLY = 4
 WARM = (512, 512, 256)
@@ -42,6 +43,7 @@ def tile_moe_eps_glu_gelu_kernel(
         keep = ctx.enter_context(tc.tile_pool(name="keep", bufs=1))
         ring = ctx.enter_context(tc.tile_pool(name="ring", bufs=E))
         lay = ctx.enter_context(tc.tile_pool(name="lay", bufs=1))
+        stage = ctx.enter_context(tc.tile_pool(name="stage", bufs=1))
         psum = ctx.enter_context(tc.psum_pool(name="psum", bufs=BANKS))
 
         offsets = keep.tile([P, S // 16], U16, name="offsets")
@@ -85,8 +87,9 @@ def tile_moe_eps_glu_gelu_kernel(
             nc.scalar.activation(out=dst[:, share // 4 :], in_=src[:, share // 4 :], func=ACT.Copy)
 
         token_words = [keep.tile([P, T], U32, name=f"token_words{s}", align_bytes=MX_ALIGN) for s in range(PASSES)]
-        slot_words = keep.tile([P, PASSES, S], U32, name="slot_words", align_bytes=MX_ALIGN)
-        slot_scales = keep.tile([P, PASSES, S], U8, name="slot_scales", align_bytes=MX_ALIGN)
+        slot_words = keep.tile([P, S + LATE * C], U32, name="slot_words", align_bytes=MX_ALIGN)
+        slot_scales = keep.tile([P, S + LATE * C], U8, name="slot_scales", align_bytes=MX_ALIGN)
+        slots = {}
 
         def quantise(s, c, grouped):
             cols = slice(HALF * c, HALF * (c + 1))
@@ -96,24 +99,33 @@ def tile_moe_eps_glu_gelu_kernel(
                 in_=grouped[:].rearrange("p w j -> p (w j)"),
             )
 
-        def gather(s, first, count):
+        def gather(s, first, words, scales):
+            count = words.shape[1] // C
             idx = offsets[:, first * C // 16 : (first + count) * C // 16]
-            cols = slice(first * C, (first + count) * C)
-            nc.vector.tensor_copy(slot_words[:, s, cols], token_words[s][:].indirect(idx))
-            nc.vector.tensor_copy(slot_scales[:, s, cols], token_scales[s][:].indirect(idx))
+            nc.vector.tensor_copy(words, token_words[s][:].indirect(idx))
+            nc.vector.tensor_copy(scales, token_scales[s][:].indirect(idx))
+            for i in range(count):
+                slots[s, first + i] = (words[:, C * i : C * (i + 1)], scales[:, C * i : C * (i + 1)])
 
         for s, raw in enumerate((raw0, raw1)):
             halves = []
             for c in range(T // HALF):
-                grouped = keep.tile([P, HALF, 4], BF16, name=f"grouped{s}{c}", tag=f"grouped{c}", align_bytes=MX_ALIGN)
+                grouped = stage.tile(
+                    [P, HALF, 4], BF16, name=f"grouped{s}{c}", align_bytes=MX_ALIGN, offset=c * HALF * 4 * 2
+                )
                 round_tokens(raw[:, :, HALF * c : HALF * (c + 1)], grouped[:], V_SHARE[s][c])
                 halves.append(grouped)
             for c, grouped in enumerate(halves):
                 quantise(s, c, grouped)
             if s == 0:
-                gather(0, 0, E)
+                gather(0, 0, slot_words[:, : LATE * C], slot_scales[:, : LATE * C])
         for first in range(0, E, 2):
-            gather(1, first, 2)
+            cols = slice((LATE + first) * C, (LATE + first + 2) * C)
+            gather(1, first, slot_words[:, cols], slot_scales[:, cols])
+        late = (E - LATE) * C
+        late_words = stage.tile([P, late], U32, name="late_words", align_bytes=MX_ALIGN, offset=HALF * 4 * 2)
+        late_scales = stage.tile([P, late], U8, name="late_scales", align_bytes=MX_ALIGN, offset=HALF * 4 * 2 + 4 * late)
+        gather(0, LATE, late_words[:], late_scales[:])
 
         def load_scales(dst, src, halved):
             rows = src.bitcast(I32).rearrange("e s (q r) i -> r q (e s) i", r=4)
@@ -152,11 +164,11 @@ def tile_moe_eps_glu_gelu_kernel(
         h_codes = {}
 
         def product(bank, m, e, s, start):
-            cols = slice(C * e, C * (e + 1))
+            words, scales = slots[s, e]
             nc.tensor.matmul_mx(
                 out=bank[:],
-                lhsT=slot_words[:, s, cols].bitcast(FP8X4),
-                lhsT_scale=slot_scales[:, s, cols],
+                lhsT=words.bitcast(FP8X4),
+                lhsT_scale=scales,
                 rhs=weights[m, e][:, s, :].bitcast(FP4X4),
                 rhs_scale=(s1, s3)[m][:, PASSES * e + s, :],
                 start=start,
@@ -229,10 +241,10 @@ def tile_moe_eps_glu_gelu_kernel(
         for width in WARM:
             nc.tensor.matmul_mx(
                 out=a_banks[0][:, :width],
-                lhsT=slot_words[:, 0, :C].bitcast(FP8X4),
-                lhsT_scale=slot_scales[:, 0, :C],
+                lhsT=slot_words[:, :C].bitcast(FP8X4),
+                lhsT_scale=slot_scales[:, :C],
                 rhs=weights[0, 0][:, 0, : 2 * width].bitcast(FP4X4),
-                rhs_scale=slot_scales[:, 0, :width],
+                rhs_scale=slot_scales[:, :width],
                 start=True,
                 stop=True,
             )

@@ -25,8 +25,8 @@ MULT = mybir.AluOpType.mult
 FLOPS = 2 * S * (2 * K * H + H * N)
 
 HALF = T // 2
-V_SHARE = ((232, 376), (160, 392))
-LATE = 4
+V_SHARE = ((232, 376), (112, 344))
+LATE = 5
 HEAD = 2
 EARLY = 4
 WARM = (512, 512, 256)

@@ -148,13 +148,10 @@ def tile_moe_eps_glu_gelu_kernel(
         w13 = w[:, :w13_bytes].rearrange("p (a s b) -> p a s b", s=PASSES, b=2 * H)
         w2 = w[:, w13_bytes:].rearrange("p (e b) -> p e b", e=E)
 
-        load_scales(s1[:], w1_scales, 0)
+        load_scales(s1[:], w1_scales, 1)
         load_scales(s3[:], w3_scales, 2)
-        for a, (m, e) in enumerate(later[:-1]):
+        for a, (m, e) in enumerate(later):
             load_weights(w13[:, a : a + 1], m, e)
-        weights[later[-1]] = w13[:, len(later) - 1]
-        for s in reversed(range(PASSES)):
-            nc.sync.dma_start(out=weights[1, E - 1][:, s, :].bitcast(I32), in_=w3_words[E - 1, s].bitcast(I32))
         nc.sync.dma_start(out=w2.bitcast(I32), in_=w2_words.bitcast(I32).rearrange("e s p b -> p (e s) b"))
         load_scales(s2[:], w2_scales, 0)
 

@@ -25,9 +25,9 @@ MULT = mybir.AluOpType.mult
 FLOPS = 2 * S * (2 * K * H + H * N)
 
 HALF = T // 2
-V_SHARE = ((232, 376), (112, 344))
-LATE = 5
-HEAD = 2
+V_SHARE = ((232, 376), (160, 392))
+LATE = 4
+HEAD = 4
 EARLY = 4
 WARM = (512, 512, 256)
 BANKS = 8
@@ -150,8 +150,12 @@ def tile_moe_eps_glu_gelu_kernel(
 
         load_scales(s1[:], w1_scales, 1)
         load_scales(s3[:], w3_scales, 2)
-        for a, (m, e) in enumerate(later):
+        for a, (m, e) in enumerate(later[:-2]):
             load_weights(w13[:, a : a + 1], m, e)
+        for e in range(E - 2, E):
+            weights[1, e] = w13[:, later.index((1, e))]
+            for s in reversed(range(PASSES)):
+                nc.sync.dma_start(out=weights[1, e][:, s, :].bitcast(I32), in_=w3_words[e, s].bitcast(I32))
         nc.sync.dma_start(out=w2.bitcast(I32), in_=w2_words.bitcast(I32).rearrange("e s p b -> p (e s) b"))
         load_scales(s2[:], w2_scales, 0)
 

@@ -25,9 +25,9 @@ MULT = mybir.AluOpType.mult
 FLOPS = 2 * S * (2 * K * H + H * N)
 
 HALF = T // 2
-V_SHARE = ((232, 376), (160, 392))
+V_SHARE = ((344, 344), (96, 272))
 LATE = 4
-HEAD = 4
+HEAD = 2
 EARLY = 4
 WARM = (512, 512, 256)
 BANKS = 8
@@ -58,11 +58,18 @@ def tile_moe_eps_glu_gelu_kernel(
         ident = keep.tile([P, P], F32, name="ident")
         make_identity(nc, ident[:])
 
-        raw0 = lay.tile([P, 4, T], F32, name="raw0", align_bytes=DMA_ALIGN, offset=0)
-        nc.sync.dma_start(out=raw0[:], in_=xT[:K_PASS, :].rearrange("(p j) w -> p j w", j=4))
-        nc.sync.dma_start(offsets[:], offs)
-        raw1 = keep.tile([P, 4, T], F32, name="raw1", align_bytes=DMA_ALIGN)
-        nc.sync.dma_start(out=raw1[:], in_=xT[K_PASS:, :].rearrange("(p j) w -> p j w", j=4))
+        raws = {}
+        for s in range(PASSES):
+            rows = xT[K_PASS * s : K_PASS * (s + 1), :].rearrange("(p j) w -> p j w", j=4)
+            for c in range(T // HALF):
+                if s == 0:
+                    raw = lay.tile([P, 4, HALF], F32, name=f"raw{s}{c}", align_bytes=DMA_ALIGN, offset=c * HALF * 16)
+                else:
+                    raw = keep.tile([P, 4, HALF], F32, name=f"raw{s}{c}", align_bytes=DMA_ALIGN)
+                nc.sync.dma_start(out=raw[:], in_=rows[:, :, HALF * c : HALF * (c + 1)])
+                raws[s, c] = raw
+                if (s, c) == (0, 0):
+                    nc.sync.dma_start(offsets[:], offs)
 
         weights = {}
 
@@ -107,15 +114,12 @@ def tile_moe_eps_glu_gelu_kernel(
             for i in range(count):
                 slots[s, first + i] = (words[:, C * i : C * (i + 1)], scales[:, C * i : C * (i + 1)])
 
-        for s, raw in enumerate((raw0, raw1)):
-            halves = []
+        for s in range(PASSES):
             for c in range(T // HALF):
                 grouped = stage.tile(
-                    [P, HALF, 4], BF16, name=f"grouped{s}{c}", align_bytes=MX_ALIGN, offset=c * HALF * 4 * 2
+                    [P, HALF, 4], BF16, name=f"grouped{s}{c}", align_bytes=MX_ALIGN, offset=(2 * s + c) * HALF * 8
                 )
-                round_tokens(raw[:, :, HALF * c : HALF * (c + 1)], grouped[:], V_SHARE[s][c])
-                halves.append(grouped)
-            for c, grouped in enumerate(halves):
+                round_tokens(raws[s, c][:], grouped[:], V_SHARE[s][c])
                 quantise(s, c, grouped)
             if s == 0:
                 gather(0, 0, slot_words[:, : LATE * C], slot_scales[:, : LATE * C])
@@ -123,8 +127,9 @@ def tile_moe_eps_glu_gelu_kernel(
             cols = slice((LATE + first) * C, (LATE + first + 2) * C)
             gather(1, first, slot_words[:, cols], slot_scales[:, cols])
         late = (E - LATE) * C
-        late_words = stage.tile([P, late], U32, name="late_words", align_bytes=MX_ALIGN, offset=HALF * 4 * 2)
-        late_scales = stage.tile([P, late], U8, name="late_scales", align_bytes=MX_ALIGN, offset=HALF * 4 * 2 + 4 * late)
+        last = 3 * HALF * 8
+        late_words = stage.tile([P, late], U32, name="late_words", align_bytes=MX_ALIGN, offset=last)
+        late_scales = stage.tile([P, late], U8, name="late_scales", align_bytes=MX_ALIGN, offset=last + 4 * late)
         gather(0, LATE, late_words[:], late_scales[:])
 
         def load_scales(dst, src, halved):
@@ -140,8 +145,8 @@ def tile_moe_eps_glu_gelu_kernel(
         s1 = lay.tile([P, E * PASSES, H], U8, name="s1", align_bytes=DMA_ALIGN, offset=0)
         s3 = lay.tile([P, E * PASSES, H], U8, name="s3", align_bytes=DMA_ALIGN, offset=scale_bytes)
         s2 = lay.tile([P, E, N], U8, name="s2", align_bytes=DMA_ALIGN, offset=2 * scale_bytes)
-        later = [(1, e) for e in range(HEAD)] + [(m, e) for e in range(HEAD, E - 2) for m in range(2)]
-        later = later + [(m, e) for m in range(2) for e in range(E - 2, E)]
+        later = [(1, e) for e in range(HEAD)]
+        later = later + [(m, e) for first in range(HEAD, E, 2) for m in range(2) for e in (first, first + 1)]
         matrix_bytes = PASSES * 2 * H
         w13_bytes = len(later) * matrix_bytes
         w = lay.tile([P, w13_bytes + E * 2 * N], U8, name="w", align_bytes=DMA_ALIGN, offset=2 * scale_bytes + E * N)
@@ -149,13 +154,12 @@ def tile_moe_eps_glu_gelu_kernel(
         w2 = w[:, w13_bytes:].rearrange("p (e b) -> p e b", e=E)
 
         load_scales(s1[:], w1_scales, 1)
-        load_scales(s3[:], w3_scales, 2)
-        for a, (m, e) in enumerate(later[:-2]):
-            load_weights(w13[:, a : a + 1], m, e)
-        for e in range(E - 2, E):
-            weights[1, e] = w13[:, later.index((1, e))]
-            for s in reversed(range(PASSES)):
-                nc.sync.dma_start(out=weights[1, e][:, s, :].bitcast(I32), in_=w3_words[e, s].bitcast(I32))
+        load_scales(s3[:], w3_scales, 1)
+        for a, (m, e) in enumerate(later):
+            if (m, e) == (0, HEAD):
+                load_weights(w13[:, a : a + 2], m, e)
+            elif (m, e) not in weights:
+                load_weights(w13[:, a : a + 1], m, e)
         nc.sync.dma_start(out=w2.bitcast(I32), in_=w2_words.bitcast(I32).rearrange("e s p b -> p (e s) b"))
         load_scales(s2[:], w2_scales, 0)
 

@@ -25,11 +25,11 @@ MULT = mybir.AluOpType.mult
 FLOPS = 2 * S * (2 * K * H + H * N)
 
 HALF = T // 2
-V_SHARE = ((344, 344), (96, 272))
-LATE = 4
+V_SHARE = ((232, 376), (112, 344))
+LATE = 5
 HEAD = 2
 EARLY = 4
-WARM = (512, 512, 256)
+WARM = (512, 256)
 BANKS = 8
 MX_ALIGN = 64
 DMA_ALIGN = 256
@@ -58,18 +58,11 @@ def tile_moe_eps_glu_gelu_kernel(
         ident = keep.tile([P, P], F32, name="ident")
         make_identity(nc, ident[:])
 
-        raws = {}
-        for s in range(PASSES):
-            rows = xT[K_PASS * s : K_PASS * (s + 1), :].rearrange("(p j) w -> p j w", j=4)
-            for c in range(T // HALF):
-                if s == 0:
-                    raw = lay.tile([P, 4, HALF], F32, name=f"raw{s}{c}", align_bytes=DMA_ALIGN, offset=c * HALF * 16)
-                else:
-                    raw = keep.tile([P, 4, HALF], F32, name=f"raw{s}{c}", align_bytes=DMA_ALIGN)
-                nc.sync.dma_start(out=raw[:], in_=rows[:, :, HALF * c : HALF * (c + 1)])
-                raws[s, c] = raw
-                if (s, c) == (0, 0):
-                    nc.sync.dma_start(offsets[:], offs)
+        raw0 = lay.tile([P, 4, T], F32, name="raw0", align_bytes=DMA_ALIGN, offset=0)
+        nc.sync.dma_start(out=raw0[:], in_=xT[:K_PASS, :].rearrange("(p j) w -> p j w", j=4))
+        nc.sync.dma_start(offsets[:], offs)
+        raw1 = keep.tile([P, 4, T], F32, name="raw1", align_bytes=DMA_ALIGN)
+        nc.sync.dma_start(out=raw1[:], in_=xT[K_PASS:, :].rearrange("(p j) w -> p j w", j=4))
 
         weights = {}
 
@@ -114,12 +107,15 @@ def tile_moe_eps_glu_gelu_kernel(
             for i in range(count):
                 slots[s, first + i] = (words[:, C * i : C * (i + 1)], scales[:, C * i : C * (i + 1)])
 
-        for s in range(PASSES):
+        for s, raw in enumerate((raw0, raw1)):
+            halves = []
             for c in range(T // HALF):
                 grouped = stage.tile(
-                    [P, HALF, 4], BF16, name=f"grouped{s}{c}", align_bytes=MX_ALIGN, offset=(2 * s + c) * HALF * 8
+                    [P, HALF, 4], BF16, name=f"grouped{s}{c}", align_bytes=MX_ALIGN, offset=c * HALF * 4 * 2
                 )
-                round_tokens(raws[s, c][:], grouped[:], V_SHARE[s][c])
+                round_tokens(raw[:, :, HALF * c : HALF * (c + 1)], grouped[:], V_SHARE[s][c])
+                halves.append(grouped)
+            for c, grouped in enumerate(halves):
                 quantise(s, c, grouped)
             if s == 0:
                 gather(0, 0, slot_words[:, : LATE * C], slot_scales[:, : LATE * C])
@@ -127,9 +123,8 @@ def tile_moe_eps_glu_gelu_kernel(
             cols = slice((LATE + first) * C, (LATE + first + 2) * C)
             gather(1, first, slot_words[:, cols], slot_scales[:, cols])
         late = (E - LATE) * C
-        last = 3 * HALF * 8
-        late_words = stage.tile([P, late], U32, name="late_words", align_bytes=MX_ALIGN, offset=last)
-        late_scales = stage.tile([P, late], U8, name="late_scales", align_bytes=MX_ALIGN, offset=last + 4 * late)
+        late_words = stage.tile([P, late], U32, name="late_words", align_bytes=MX_ALIGN, offset=HALF * 4 * 2)
+        late_scales = stage.tile([P, late], U8, name="late_scales", align_bytes=MX_ALIGN, offset=HALF * 4 * 2 + 4 * late)
         gather(0, LATE, late_words[:], late_scales[:])
 
         def load_scales(dst, src, halved):
@@ -145,8 +140,8 @@ def tile_moe_eps_glu_gelu_kernel(
         s1 = lay.tile([P, E * PASSES, H], U8, name="s1", align_bytes=DMA_ALIGN, offset=0)
         s3 = lay.tile([P, E * PASSES, H], U8, name="s3", align_bytes=DMA_ALIGN, offset=scale_bytes)
         s2 = lay.tile([P, E, N], U8, name="s2", align_bytes=DMA_ALIGN, offset=2 * scale_bytes)
-        later = [(1, e) for e in range(HEAD)]
-        later = later + [(m, e) for first in range(HEAD, E, 2) for m in range(2) for e in (first, first + 1)]
+        later = [(1, e) for e in range(HEAD)] + [(m, e) for e in range(HEAD, E - 2) for m in range(2)]
+        later = later + [(m, e) for m in range(2) for e in range(E - 2, E)]
         matrix_bytes = PASSES * 2 * H
         w13_bytes = len(later) * matrix_bytes
         w = lay.tile([P, w13_bytes + E * 2 * N], U8, name="w", align_bytes=DMA_ALIGN, offset=2 * scale_bytes + E * N)
@@ -154,12 +149,9 @@ def tile_moe_eps_glu_gelu_kernel(
         w2 = w[:, w13_bytes:].rearrange("p (e b) -> p e b", e=E)
 
         load_scales(s1[:], w1_scales, 1)
-        load_scales(s3[:], w3_scales, 1)
+        load_scales(s3[:], w3_scales, 2)
         for a, (m, e) in enumerate(later):
-            if (m, e) == (0, HEAD):
-                load_weights(w13[:, a : a + 2], m, e)
-            elif (m, e) not in weights:
-                load_weights(w13[:, a : a + 1], m, e)
+            load_weights(w13[:, a : a + 1], m, e)
         nc.sync.dma_start(out=w2.bitcast(I32), in_=w2_words.bitcast(I32).rearrange("e s p b -> p (e s) b"))
         load_scales(s2[:], w2_scales, 0)
 
@@ -180,6 +172,17 @@ def tile_moe_eps_glu_gelu_kernel(
                 stop=not start,
             )
 
+        def warm_up(bank, words, width):
+            nc.tensor.matmul_mx(
+                out=bank[:, :width],
+                lhsT=words.bitcast(FP8X4),
+                lhsT_scale=slot_scales[:, :C],
+                rhs=weights[0, 0][:, 0, : 2 * width].bitcast(FP4X4),
+                rhs_scale=slot_scales[:, :width],
+                start=True,
+                stop=True,
+            )
+
         def gate(e):
             g = ring.tile([P, H], F32, name="g")
             nc.scalar.activation(
@@ -190,7 +193,7 @@ def tile_moe_eps_glu_gelu_kernel(
             gelus[e] = g
 
         def hidden(e):
-            b = psum.tile([P, H], F32, name="b", tag="bank")
+            b = first_b if e == 0 else psum.tile([P, H], F32, name="b", tag="bank")
             product(b, 1, e, 1, True)
             product(b, 1, e, 0, False)
             h = ring.tile([P, H], BF16, name="h")
@@ -244,17 +247,11 @@ def tile_moe_eps_glu_gelu_kernel(
         for e in range(HEAD):
             a_banks[e] = psum.tile([P, H], F32, name="a", tag="bank")
         for width in WARM:
-            nc.tensor.matmul_mx(
-                out=a_banks[0][:, :width],
-                lhsT=slot_words[:, :C].bitcast(FP8X4),
-                lhsT_scale=slot_scales[:, :C],
-                rhs=weights[0, 0][:, 0, : 2 * width].bitcast(FP4X4),
-                rhs_scale=slot_scales[:, :width],
-                start=True,
-                stop=True,
-            )
+            warm_up(a_banks[0], slot_words[:, :C], width)
         for e in range(HEAD):
             product(a_banks[e], 0, e, 0, True)
+        first_b = psum.tile([P, H], F32, name="b", tag="bank")
+        warm_up(first_b, slots[1, 0][0], H)
         for e in range(HEAD):
             product(a_banks[e], 0, e, 1, False)
             gate(e)

@@ -205,19 +205,18 @@ def tile_moe_eps_glu_gelu_kernel(
             )
             hs[e] = h
 
-        def turn(experts, copy):
+        def turn(experts, copies):
             count = len(experts)
-            turned = psum.tile([P, H], F32, name="turned", tag="bank")
-            for i, e in enumerate(experts):
-                for u in range(2):
-                    at = P * (2 * i + u)
-                    words = hs[e][:].bitcast(F32)[:, P * u : P * (u + 1)]
-                    nc.tensor.transpose(turned[:, at : at + P], words, ident[:])
             h_grouped = keep.tile([P, count * C, 4], BF16, name=f"h_grouped{experts[0]}", align_bytes=MX_ALIGN)
-            copy(
-                out=h_grouped[:].bitcast(F32).rearrange("p (i r) u -> p i r u", i=count),
-                in_=turned[:, : 2 * count * P].rearrange("p (i u r) -> p i r u", i=count, u=2),
-            )
+            for i, e in enumerate(experts):
+                turned = psum.tile([P, H], F32, name="turned", tag="bank")
+                for u in range(2):
+                    words = hs[e][:].bitcast(F32)[:, P * u : P * (u + 1)]
+                    nc.tensor.transpose(turned[:, P * u : P * (u + 1)], words, ident[:])
+                copies[i](
+                    out=h_grouped[:, C * i : C * (i + 1)].bitcast(F32),
+                    in_=turned[:, : 2 * P].rearrange("p (u r) -> p r u", u=2),
+                )
             h_words = keep.tile([P, count * C], U32, name=f"h_words{experts[0]}", align_bytes=MX_ALIGN)
             h_scales = keep.tile([P, count * C], U8, name=f"h_scales{experts[0]}", align_bytes=MX_ALIGN)
             nc.vector.quantize_mx(
@@ -264,17 +263,17 @@ def tile_moe_eps_glu_gelu_kernel(
                 gate(e)
             else:
                 hidden(e)
-        turn((0, 1), scalar_copy)
-        turn((2,), vector_copy)
-        turn((3, 4), scalar_copy)
-        turn((5,), scalar_copy)
+        turn((0, 1), (scalar_copy, scalar_copy))
+        turn((2, 3), (vector_copy, scalar_copy))
+        turn((4,), (scalar_copy,))
+        turn((5,), (scalar_copy,))
 
         def fresh():
             return psum.tile([P, H], F32, name="y", tag="bank")
 
         parts = (
-            (((0, 1, 2), scalar_copy), ((3, 4), scalar_copy), ((5,), vector_copy)),
-            (((0, 1, 2), vector_copy), ((3, 4, 5), scalar_copy)),
+            (((0, 1), scalar_copy), ((2, 3), scalar_copy), ((4,), vector_copy), ((5,), vector_copy)),
+            (((0, 1, 2, 3), scalar_copy), ((4, 5), vector_copy)),
         )
         for t in range(N // P):
             result = keep.tile([P, R, E * RU], F32, name=f"result{t}", align_bytes=DMA_ALIGN)

@@ -127,10 +127,10 @@ def tile_moe_eps_glu_gelu_kernel(
         late_scales = stage.tile([P, late], U8, name="late_scales", align_bytes=MX_ALIGN, offset=HALF * 4 * 2 + 4 * late)
         gather(0, LATE, late_words[:], late_scales[:])
 
-        def load_scales(dst, src, halved):
+        def load_scales(dst, src, halved=()):
             rows = src.bitcast(I32).rearrange("e s (q r) i -> r q (e s) i", r=4)
             for r in range(4):
-                parts = 2 if r >= 4 - halved else 1
+                parts = 2 if r in halved else 1
                 width = dst.shape[1] // parts
                 for part in range(parts):
                     at = slice(width * part, width * (part + 1))
@@ -148,12 +148,12 @@ def tile_moe_eps_glu_gelu_kernel(
         w13 = w[:, :w13_bytes].rearrange("p (a s b) -> p a s b", s=PASSES, b=2 * H)
         w2 = w[:, w13_bytes:].rearrange("p (e b) -> p e b", e=E)
 
-        load_scales(s1[:], w1_scales, 1)
-        load_scales(s3[:], w3_scales, 2)
+        load_scales(s1[:], w1_scales, (0,))
+        load_scales(s3[:], w3_scales, (2, 3))
         for a, (m, e) in enumerate(later):
             load_weights(w13[:, a : a + 1], m, e)
         nc.sync.dma_start(out=w2.bitcast(I32), in_=w2_words.bitcast(I32).rearrange("e s p b -> p (e s) b"))
-        load_scales(s2[:], w2_scales, 0)
+        load_scales(s2[:], w2_scales)
 
         a_banks = {}
         gelus = {}

from contextlib import ExitStack

import concourse.mybir as mybir
from concourse.masks import make_identity

K, T, E, C, H, N = 1024, 1024, 6, 128, 512, 256
R = 4
S = E * C
P = 128
K_PASS = 4 * P
PASSES = K // K_PASS
RU = C // R

F32 = mybir.dt.float32
BF16 = mybir.dt.bfloat16
I32 = mybir.dt.int32
U32 = mybir.dt.uint32
U16 = mybir.dt.uint16
U8 = mybir.dt.uint8
FP8X4 = mybir.dt.float8_e4m3fn_x4
FP4X4 = mybir.dt.float4_e2m1fn_x4
ACT = mybir.ActivationFunctionType
MULT = mybir.AluOpType.mult

FLOPS = 2 * S * (2 * K * H + H * N)

HALF = T // 2
V_SHARE = ((232, 376), (112, 344))
LATE = 5
HEAD = 2
EARLY = 4
WARM = (512, 256)
BANKS = 8
MX_ALIGN = 64
DMA_ALIGN = 256


def tile_moe_eps_glu_gelu_kernel(
    tc, xT, w1_words, w1_scales, w3_words, w3_scales, w2_words, w2_scales, offs, out
):
    nc = tc.nc
    with ExitStack() as ctx:
        keep = ctx.enter_context(tc.tile_pool(name="keep", bufs=1))
        ring = ctx.enter_context(tc.tile_pool(name="ring", bufs=E))
        lay = ctx.enter_context(tc.tile_pool(name="lay", bufs=1))
        stage = ctx.enter_context(tc.tile_pool(name="stage", bufs=1))
        psum = ctx.enter_context(tc.psum_pool(name="psum", bufs=BANKS))

        offsets = keep.tile([P, S // 16], U16, name="offsets")

        token_scales = [keep.tile([P, T], U8, name=f"token_scales{s}", align_bytes=MX_ALIGN) for s in range(PASSES)]
        zero = keep.tile([P, 1], F32, name="zero")
        warm = keep.tile([P, 1], F32, name="warm")
        nc.vector.memset(zero[:], 0.0)
        for tile in token_scales:
            nc.vector.memset(tile[:].bitcast(I32), 0)
        nc.scalar.activation(out=warm[:], in_=zero[:], func=ACT.Gelu_apprx_tanh)
        ident = keep.tile([P, P], F32, name="ident")
        make_identity(nc, ident[:])

        raw0 = lay.tile([P, 4, T], F32, name="raw0", align_bytes=DMA_ALIGN, offset=0)
        nc.sync.dma_start(out=raw0[:], in_=xT[:K_PASS, :].rearrange("(p j) w -> p j w", j=4))
        nc.sync.dma_start(offsets[:], offs)
        raw1 = keep.tile([P, 4, T], F32, name="raw1", align_bytes=DMA_ALIGN)
        nc.sync.dma_start(out=raw1[:], in_=xT[K_PASS:, :].rearrange("(p j) w -> p j w", j=4))

        weights = {}

        def load_weights(dst, m, first):
            count = dst.shape[1]
            src = (w1_words, w3_words)[m][first : first + count]
            nc.sync.dma_start(
                out=dst.bitcast(I32).rearrange("p e s b -> p (e s) b"),
                in_=src.bitcast(I32).rearrange("e s p b -> p (e s) b"),
            )
            for i in range(count):
                weights[m, first + i] = dst[:, i]

        head = keep.tile([P, HEAD, PASSES, 2 * H], U8, name="head", align_bytes=DMA_ALIGN)
        load_weights(head[:], 0, 0)

        def round_tokens(src, dst, share):
            src = src.rearrange("p j (w i) -> p w j i", i=4)
            dst = dst.rearrange("p (w i) j -> p w j i", i=4)
            if share:
                nc.vector.tensor_copy(out=dst[:, : share // 4], in_=src[:, : share // 4])
            nc.scalar.activation(out=dst[:, share // 4 :], in_=src[:, share // 4 :], func=ACT.Copy)

        token_words = [keep.tile([P, T], U32, name=f"token_words{s}", align_bytes=MX_ALIGN) for s in range(PASSES)]
        slot_words = keep.tile([P, S + LATE * C], U32, name="slot_words", align_bytes=MX_ALIGN)
        slot_scales = keep.tile([P, S + LATE * C], U8, name="slot_scales", align_bytes=MX_ALIGN)
        slots = {}

        def quantise(s, c, grouped):
            cols = slice(HALF * c, HALF * (c + 1))
            nc.vector.quantize_mx(
                out=token_words[s][:, cols].bitcast(FP8X4),
                scales=token_scales[s][:, cols],
                in_=grouped[:].rearrange("p w j -> p (w j)"),
            )

        def gather(s, first, words, scales):
            count = words.shape[1] // C
            idx = offsets[:, first * C // 16 : (first + count) * C // 16]
            nc.vector.tensor_copy(words, token_words[s][:].indirect(idx))
            nc.vector.tensor_copy(scales, token_scales[s][:].indirect(idx))
            for i in range(count):
                slots[s, first + i] = (words[:, C * i : C * (i + 1)], scales[:, C * i : C * (i + 1)])

        for s, raw in enumerate((raw0, raw1)):
            halves = []
            for c in range(T // HALF):
                grouped = stage.tile(
                    [P, HALF, 4], BF16, name=f"grouped{s}{c}", align_bytes=MX_ALIGN, offset=c * HALF * 4 * 2
                )
                round_tokens(raw[:, :, HALF * c : HALF * (c + 1)], grouped[:], V_SHARE[s][c])
                halves.append(grouped)
            for c, grouped in enumerate(halves):
                quantise(s, c, grouped)
            if s == 0:
                gather(0, 0, slot_words[:, : LATE * C], slot_scales[:, : LATE * C])
        for first in range(0, E, 2):
            cols = slice((LATE + first) * C, (LATE + first + 2) * C)
            gather(1, first, slot_words[:, cols], slot_scales[:, cols])
        late = (E - LATE) * C
        late_words = stage.tile([P, late], U32, name="late_words", align_bytes=MX_ALIGN, offset=HALF * 4 * 2)
        late_scales = stage.tile([P, late], U8, name="late_scales", align_bytes=MX_ALIGN, offset=HALF * 4 * 2 + 4 * late)
        gather(0, LATE, late_words[:], late_scales[:])

        def load_scales(dst, src, halved=()):
            rows = src.bitcast(I32).rearrange("e s (q r) i -> r q (e s) i", r=4)
            for r in range(4):
                parts = 2 if r in halved else 1
                width = dst.shape[1] // parts
                for part in range(parts):
                    at = slice(width * part, width * (part + 1))
                    nc.sync.dma_start(out=dst.bitcast(I32)[r:P:32, at], in_=rows[r][:, at])

        scale_bytes = E * PASSES * H
        s1 = lay.tile([P, E * PASSES, H], U8, name="s1", align_bytes=DMA_ALIGN, offset=0)
        s3 = lay.tile([P, E * PASSES, H], U8, name="s3", align_bytes=DMA_ALIGN, offset=scale_bytes)
        s2 = lay.tile([P, E, N], U8, name="s2", align_bytes=DMA_ALIGN, offset=2 * scale_bytes)
        later = [(1, e) for e in range(HEAD)] + [(m, e) for e in range(HEAD, E - 2) for m in range(2)]
        later = later + [(m, e) for m in range(2) for e in range(E - 2, E)]
        matrix_bytes = PASSES * 2 * H
        w13_bytes = len(later) * matrix_bytes
        w = lay.tile([P, w13_bytes + E * 2 * N], U8, name="w", align_bytes=DMA_ALIGN, offset=2 * scale_bytes + E * N)
        w13 = w[:, :w13_bytes].rearrange("p (a s b) -> p a s b", s=PASSES, b=2 * H)
        w2 = w[:, w13_bytes:].rearrange("p (e b) -> p e b", e=E)

        load_scales(s1[:], w1_scales, (0,))
        load_scales(s3[:], w3_scales, (2, 3))
        for a, (m, e) in enumerate(later):
            load_weights(w13[:, a : a + 1], m, e)
        nc.sync.dma_start(out=w2.bitcast(I32), in_=w2_words.bitcast(I32).rearrange("e s p b -> p (e s) b"))
        load_scales(s2[:], w2_scales)

        a_banks = {}
        gelus = {}
        hs = {}
        h_codes = {}

        def product(bank, m, e, s, start):
            words, scales = slots[s, e]
            nc.tensor.matmul_mx(
                out=bank[:],
                lhsT=words.bitcast(FP8X4),
                lhsT_scale=scales,
                rhs=weights[m, e][:, s, :].bitcast(FP4X4),
                rhs_scale=(s1, s3)[m][:, PASSES * e + s, :],
                start=start,
                stop=not start,
            )

        def warm_up(bank, words, width):
            nc.tensor.matmul_mx(
                out=bank[:, :width],
                lhsT=words.bitcast(FP8X4),
                lhsT_scale=slot_scales[:, :C],
                rhs=weights[0, 0][:, 0, : 2 * width].bitcast(FP4X4),
                rhs_scale=slot_scales[:, :width],
                start=True,
                stop=True,
            )

        def gate(e):
            g = ring.tile([P, H], F32, name="g")
            nc.scalar.activation(
                out=g[:].rearrange("p (u q d) -> p u q d", u=2, d=2),
                in_=a_banks[e][:].rearrange("p (q u d) -> p u q d", u=2, d=2),
                func=ACT.Gelu_apprx_tanh,
            )
            gelus[e] = g

        def hidden(e):
            b = first_b if e == 0 else psum.tile([P, H], F32, name="b", tag="bank")
            product(b, 1, e, 1, True)
            product(b, 1, e, 0, False)
            h = ring.tile([P, H], BF16, name="h")
            nc.vector.tensor_tensor(
                h[:].rearrange("p (u q d) -> p u q d", u=2, d=2),
                b[:].rearrange("p (q u d) -> p u q d", u=2, d=2),
                gelus[e][:].rearrange("p (u q d) -> p u q d", u=2, d=2),
                MULT,
            )
            hs[e] = h

        def turn(experts, copies):
            count = len(experts)
            h_grouped = keep.tile([P, count * C, 4], BF16, name=f"h_grouped{experts[0]}", align_bytes=MX_ALIGN)
            for i, e in enumerate(experts):
                turned = psum.tile([P, H], F32, name="turned", tag="bank")
                for u in range(2):
                    words = hs[e][:].bitcast(F32)[:, P * u : P * (u + 1)]
                    nc.tensor.transpose(turned[:, P * u : P * (u + 1)], words, ident[:])
                copies[i](
                    out=h_grouped[:, C * i : C * (i + 1)].bitcast(F32),
                    in_=turned[:, : 2 * P].rearrange("p (u r) -> p r u", u=2),
                )
            h_words = keep.tile([P, count * C], U32, name=f"h_words{experts[0]}", align_bytes=MX_ALIGN)
            h_scales = keep.tile([P, count * C], U8, name=f"h_scales{experts[0]}", align_bytes=MX_ALIGN)
            nc.vector.quantize_mx(
                out=h_words[:].bitcast(FP8X4), scales=h_scales[:], in_=h_grouped[:].rearrange("p c t -> p (c t)")
            )
            for i, e in enumerate(experts):
                h_codes[e] = (h_words[:, C * i : C * (i + 1)], h_scales[:, C * i : C * (i + 1)])

        def second_layer(experts, t, bank, copy, dst):
            y = bank[:, : len(experts) * C].rearrange("p (i c) -> p i c", c=C)
            for i, e in enumerate(experts):
                h_words, h_scales = h_codes[e]
                nc.tensor.matmul_mx(
                    out=y[:, i, :],
                    lhsT=w2[:, e, 2 * P * t : 2 * P * (t + 1)].bitcast(FP4X4),
                    lhsT_scale=s2[:, e, P * t : P * (t + 1)],
                    rhs=h_words.bitcast(FP8X4),
                    rhs_scale=h_scales,
                    start=True,
                    stop=True,
                )
            copy(
                out=dst.rearrange("p m (i u) -> p m i u", i=len(experts)),
                in_=y.rearrange("p i (m u) -> p m i u", m=R),
            )

        for e in range(HEAD):
            a_banks[e] = psum.tile([P, H], F32, name="a", tag="bank")
        for width in WARM:
            warm_up(a_banks[0], slot_words[:, :C], width)
        for e in range(HEAD):
            product(a_banks[e], 0, e, 0, True)
        first_b = psum.tile([P, H], F32, name="b", tag="bank")
        warm_up(first_b, slots[1, 0][0], H)
        for e in range(HEAD):
            product(a_banks[e], 0, e, 1, False)
            gate(e)
        scalar_copy, vector_copy = nc.scalar.copy, nc.vector.tensor_copy
        for m, e in later:
            if m == 0:
                a_banks[e] = psum.tile([P, H], F32, name="a", tag="bank")
                product(a_banks[e], 0, e, 1, True)
                product(a_banks[e], 0, e, 0, False)
                gate(e)
            else:
                hidden(e)
        turn((0, 1), (scalar_copy, scalar_copy))
        turn((2, 3), (vector_copy, scalar_copy))
        turn((4,), (scalar_copy,))
        turn((5,), (scalar_copy,))

        def fresh():
            return psum.tile([P, H], F32, name="y", tag="bank")

        parts = (
            (((0, 1), scalar_copy), ((2, 3), scalar_copy), ((4,), vector_copy), ((5,), vector_copy)),
            (((0, 1, 2, 3), scalar_copy), ((4, 5), vector_copy)),
        )
        for t in range(N // P):
            result = keep.tile([P, R, E * RU], F32, name=f"result{t}", align_bytes=DMA_ALIGN)
            for experts, copy in parts[t]:
                second_layer(experts, t, fresh(), copy, result[:, :, experts[0] * RU : (experts[-1] + 1) * RU])
            nc.sync.dma_start(out=out[P * t : P * (t + 1), :], in_=result[:].rearrange("p m x -> p (m x)"))
